import numpy as np, ml_dtypes
CORES = [35,38,43,46]
N = 4
import mx_ref
BF = ml_dtypes.bfloat16
def cols(t, e):
    v = np.concatenate([t.reshape(128, -1, 4), np.zeros((128, 1, 4), BF)], axis=1)
    return np.ascontiguousarray(v[:, e]).reshape(128, -1)
def pick(q, e):
    c = np.concatenate([q[0].reshape(128, -1, 4), np.zeros((128, 1, 4), np.uint8)], axis=1); s = np.concatenate([q[1], np.ones((16, 1), np.uint8)], axis=1)
    return (np.ascontiguousarray(c[:, e].reshape(128, -1)), np.ascontiguousarray(s[:, e]))
def join(*qs):
    return (np.concatenate([q[0] for q in qs], axis=1), np.concatenate([q[1] for q in qs], axis=1))
def put(q, e, v):
    c, s = q[0].reshape(128, -1, 4).copy(), q[1].copy(); c[:, e] = v[0].reshape(128, -1, 4); s[:, e] = v[1]
    return (c.reshape(128, -1), s)
def pk(c, s):
    return (np.ascontiguousarray(c), mx_ref.live(s))
def emit(q):
    return q[0], q[1]
def decode(q):
    o = []
    for b in range(4):
        e = np.zeros((128, 128, 4), np.float32); e[np.arange(128), np.arange(128), b] = 1
        o.append(mx_ref.matmul(mx_ref.quantize(e.reshape(128, 512).astype(BF)), q))
    return np.stack(o, axis=2).reshape(128, -1)
def f(rng, *shape):
    return mx_ref.flush((rng.standard_normal(shape, dtype=np.float32) * np.exp2(rng.integers(-2, 3, shape[:-1] + (1,)))).astype(BF))
def wide(rng, *shape, cols=0):
    v = rng.standard_normal(shape, dtype=np.float32) * np.exp2(rng.integers(-12, 13, shape)).astype(np.float32)
    if cols: v *= np.repeat(np.exp2(rng.integers(-cols, cols + 1, shape[:-2] + (1, shape[-1] // 4))) * (rng.random(shape[:-2] + (1, shape[-1] // 4)) > 0.0625), 4, axis=-1).astype(np.float32)
    return mx_ref.flush(v.astype(BF))
T, L, PL, R = 384, 64, 6, 3
def sized(v, k):
    v = v.astype(np.float32) * np.float32(k)
    v[np.abs(v) < np.float32(2.0 ** -6)] = 0
    return v.astype(BF)
def column(w, k, v):
    w[:, :, 4 * k:4 * k + 4] = np.asarray(v, np.float32).astype(BF)
def plain(rng):
    return {"x": sized(f(rng, N, 128, 4 * T), 16), "w": np.repeat(f(rng, 1, 128, 512), N, axis=0), "z": f(rng, N, 128, 512)}
def setup_inputs(rng):
    return plain(rng)
def setup_inputs_steps(rng):
    d = plain(rng)
    d["w"][:, 96:] = 0
    for t in range(R):
        v = np.zeros((128, 4))
        v[0, 0], v[64, 0] = 1.0, 2.0 ** -21
        column(d["w"], 8 * t + 6, v)
        for i in range(PL): d["w"][:, 64, 4 * (8 * t + i)] = 0
    x = d["x"].reshape(N, 128, T, 4).astype(np.float32)
    x[:, :96] = np.tile(x[:, :96, :T // 4], (1, 1, 4, 1))
    x[:, 64, :, 0] = np.repeat([5.0, 6.0, 7.0, 7.0], T // 4)
    x[:, 0, :, 0] = np.where(np.arange(N) % 2 == 0, 4.0, -4.0)[:, None]
    d["x"] = x.reshape(N, 128, 4 * T).astype(BF)
    return d
def setup_inputs_far(rng):
    d = plain(rng)
    g = 1 - 2 * rng.integers(0, 2, (N, T))
    g[::2] = 1
    v = (1.5 + 0.5 * rng.random((N, 128, 4 * T), dtype=np.float32)) * np.float32(2.0 ** 27)
    d["x"] = (v * np.repeat(g, 4, axis=1)[:, None, :].astype(np.float32)).astype(BF)
    for t in range(R):
        for i in range(PL):
            column(d["w"], 8 * t + i, np.repeat([-1.0, 1.0], 256)[rng.permutation(512)].reshape(128, 4))
        column(d["w"], 8 * t + 6, -(2.0 ** 30) * rng.choice([0.875, 1.0], (128, 4)))
    return d
def setup_inputs_cancel(rng):
    d = plain(rng)
    d["w"][:, 64:] = 0
    d["x"][:, :64, :4] = d["x"][0, :64, :4].astype(np.float32).astype(BF)
    v = rng.integers(4, 8, (64, 4)) * 2.0 ** 22 * rng.choice([-1.0, 1.0], (64, 4))
    k = [1.0, 2.0 ** -26, -1.0, 2.0 ** -26]
    for r in range(N):
        d["x"][r, 64:] = np.tile(v * k[r % 4], (1, T)).astype(np.float32).astype(BF)
    return d
def setup_inputs_bare(rng):
    d = plain(rng)
    a, b = [int(i) for i in rng.permutation(N)[:2]]
    d["x"][:, 127, ::4] = 0
    one = d["x"][a, :, :4].astype(np.float32)
    k = np.repeat(np.exp2(rng.integers(0, 4, T)), 4).astype(np.float32)
    d["x"][a] = (np.tile(one, (1, T)) * k).astype(BF)
    e = np.where(rng.permutation(T) % 4 > 0, -1, np.arange(T))
    d["x"][b] = cols(d["x"][b], e)
    d["x"][b, 127, 4 * np.flatnonzero(e >= 0)] = 65536.0
    for i in range(PL): d["w"][:, 127, 4 * i] = 1.0
    d["w"][:, 127, 4 * 6] = -1.0
    for i in range(PL): column(d["w"], 8 + i, 0)
    column(d["w"], 8 * (R - 1) + 6, 0)
    return d
def setup_inputs_spread(rng):
    return {**plain(rng), "x": sized(wide(rng, N, 128, 4 * T, cols=6), 64)}
def check_inputs(d):
    b = []
    for k, low, high in (("x", 2.0 ** -6, 2.0 ** 28), ("w", 2.0 ** -30, 2.0 ** 30), ("z", 2.0 ** -30, 2.0 ** 30)):
        v = np.abs(d[k].astype(np.float32))
        if not (np.isfinite(v).all() and ((v == 0) | (v >= low) & (v <= high)).all()): b.append("a value of " + k)
    w = d["w"].astype(np.float32)
    if (w != w[:1]).any(): b.append("w differs from rank to rank")
    return b
def reference(x, w, z):
    y, lv = np.zeros((N, 128, T), np.float32), np.zeros((N, R, T), np.float32)
    oc, osc = np.zeros((N, 128, 4 * T), np.uint8), np.zeros((N, 16, T), np.uint8)
    state = [mx_ref.quantize(np.ascontiguousarray(x[r])) for r in range(N)]
    wq = [mx_ref.quantize(np.ascontiguousarray(w[r])) for r in range(N)]
    for t in range(R):
        leaf, have = np.zeros((N, T), int), []
        total = np.zeros((128, L, 4), np.float32)
        for r in range(N):
            p = mx_ref.matmul(wq[r], state[r])[8 * t:8 * t + 7] + np.float32(0)
            have.append(decode(state[r]).reshape(128, T, 4))
            for i in range(PL): leaf[r] += (p[i] < 0) * (1 << i)
            for l in range(L):
                m = np.flatnonzero(leaf[r] == l)
                if m.size: total[:, l] = total[:, l] + have[r][:, m[np.argmax(p[6, m])]]
        v = mx_ref.quantize(np.ascontiguousarray((total * np.float32(0.125)).reshape(128, 4 * L).astype(BF)))
        v = decode(v).reshape(128, L, 4)
        for r in range(N):
            new = have[r] - v[:, leaf[r]] * np.float32(0.5)
            state[r] = mx_ref.quantize(np.ascontiguousarray(new.reshape(128, 4 * T).astype(BF)))
            lv[r, t] = leaf[r]
    for r in range(N):
        y[r] = mx_ref.matmul(mx_ref.quantize(np.ascontiguousarray(z[r])), state[r])
        oc[r], osc[r] = emit(state[r])
    return {"y": y, "oc": oc, "osc": osc, "lv": lv}

@@ -1,0 +1,418 @@
+from concourse.bass import DstId, RemoteDMATransfer
+from concourse.mybir import dt, AluOpType, AxisListType, ActivationFunctionType
+
+ALU = AluOpType
+ACT = ActivationFunctionType
+R, L, TC, H, PAD = 3, 64, 384, 192, 2
+X4, U8, BF, F32, I32, U16 = "float8_e4m3fn_x4", "uint8", "bfloat16", "float32", "int32", "uint16"
+
+SCRATCH = {
+    "psa": ("psum", [128, 2048], F32), "psb": ("psum", [128, 2048], F32),
+    "tw": ("sbuf", [128, 4 * 580], BF), "hx": ("sbuf", [128, 4 * (TC + PAD)], BF),
+    "bt": ("sbuf", [128, 4 * H], BF), "cg": ("sbuf", [128, 512], BF), "ci": ("sbuf", [128, 512], BF),
+    "cl": ("sbuf", [128, 512], BF), "et": ("sbuf", [128, 520], BF), "et2": ("sbuf", [128, 520], BF),
+    "vt": ("sbuf", [128, 512], BF), "zt": ("sbuf", [128, 512], BF), "m16": ("sbuf", [128, H], BF),
+    "junk": ("sbuf", [128, H + PAD], BF),
+    "aip": ("sbuf", [128, 8], I32), "aik": ("sbuf", [128, 8], I32), "im": ("sbuf", [128, L], I32),
+    "iv": ("sbuf", [128, L], I32),
+    "iv2": ("sbuf", [128, L], I32), "i16": ("sbuf", [128, H], I32), "a16": ("sbuf", [128, H], I32),
+    "ipen": ("sbuf", [128, 4], I32), "apen": ("sbuf", [128, 4], I32), "lc": ("sbuf", [128, 12], I32),
+    "li": ("sbuf", [128, 24], I32),
+    "f1": ("sbuf", [128, 8], F32), "f2": ("sbuf", [128, 8], F32), "col": ("sbuf", [128, 32], F32),
+    "pen": ("sbuf", [128, 4], F32), "mc": ("sbuf", [128, 4], F32), "sp": ("sbuf", [128, H], F32),
+    "key": ("sbuf", [128, H], F32), "run": ("sbuf", [128, H + PAD], F32), "cnt": ("sbuf", [128, 8], F32),
+    "d0": ("sbuf", [128, H], F32), "ls": ("sbuf", [128, H], F32), "lf": ("sbuf", [128, 32], F32),
+    "lt": ("sbuf", [128, 32], F32), "ysb": ("sbuf", [128, TC], F32), "dl": ("sbuf", [128, 4 * L], F32),
+}
+
+
+def _pair(name, n):
+    SCRATCH[name + "q"] = ("sbuf", [128, n], X4)
+    SCRATCH[name + "s"] = ("sbuf", [128, n], U8)
+
+
+for _n, _w in (("w", 576), ("b", H), ("i", 128), ("cg", 128), ("ci", 128), ("cl", 128), ("e", 512), ("f", 512), ("z", 128)):
+    _pair("k" + _n, _w)
+for _t in range(R + 1):
+    _pair("st%d" % _t, TC + PAD)
+for _t in range(R):
+    _pair("rep%d" % _t, 192)
+    _pair("land%d" % _t, 320)
+    _pair("val%d" % _t, 128)
+    _pair("sel%d" % _t, TC)
+    SCRATCH["ofr%d" % _t] = ("sbuf", [128, 4], U16)
+    SCRATCH["ofl%d" % _t] = ("sbuf", [128, 24], U16)
+
+NC, ND = 110, 22
+SEMAPHORES = (["c%d" % k for k in range(NC)] + ["d%d" % k for k in range(ND)]
+              + ["arr%d_%d" % (t, r) for t in range(R) for r in range(4)] + ["sent"])
+
+BIT = 2.0 ** 26
+FLOOR = -2.0 ** 51
+MAGIC = 1.5 * 2.0 ** 27
+
+
+def engine_sets(src, cores, topo):
+    peers = [c for c in cores if c != src]
+    far = [c for c in peers if topo.chip(c) != topo.chip(src)]
+    near = [c for c in peers if topo.chip(c) == topo.chip(src)]
+    out = {}
+    used = []
+    if far:
+        used = topo.engines(src, far[0])
+        k = len(used) // len(far)
+        for n, c in enumerate(far):
+            out[c] = used[n * k:(n + 1) * k]
+    if near:
+        rest = [e for e in topo.engines(src, near[0]) if e not in used]
+        k = len(rest) // len(near)
+        for n, c in enumerate(near):
+            out[c] = rest[n * k:(n + 1) * k]
+    return out
+
+
+def emit_program(ops, queues, T):
+    writer, readers, known, issue, closure, waits, before = {}, {}, {}, [], [], [], {}
+    for n, o in enumerate(ops):
+        deps = set()
+        for k in o["r"]:
+            if k in writer: deps.add(writer[k])
+        for k in o["w"]:
+            if k in writer: deps.add(writer[k])
+            deps.update(readers.get(k, ()))
+        if o["cont"]:
+            deps.discard(writer[o["w"][0]])
+        kn = known.setdefault(o["q"], set())
+        mine = []
+        for d in sorted(deps, reverse=True):
+            if d not in kn:
+                mine.append(d)
+                kn.add(d)
+                kn.update(closure[d])
+        waits.append(mine[::-1])
+        issue.append(set(kn))
+        c = set(kn)
+        if not o["dma"]:
+            if o["q"] in before:
+                c.add(before[o["q"]])
+                c.update(closure[before[o["q"]]])
+            before[o["q"]] = n
+        closure.append(c)
+        for k in o["r"]: readers.setdefault(k, []).append(n)
+        for k in o["w"]:
+            writer[k] = n
+            readers[k] = []
+    signalled = set()
+    for m in waits: signalled.update(m)
+    pools = {False: ["c%d" % k for k in range(NC)], True: ["d%d" % k for k in range(ND)]}
+    last, count, where = {}, {}, {}
+    for n, o in enumerate(ops):
+        q = queues[o["q"]]
+        for d in waits[n]:
+            q.wait_ge(T.sem[where[d][0]], where[d][1])
+        for name, val in o["extra"]:
+            q.wait_ge(T.sem[name], val)
+        if o["f"] is None:
+            continue
+        ins = o["f"]()
+        if n in signalled:
+            name = [s for s in pools[o["dma"]] if s not in last or last[s] in issue[n]][0]
+            step = 16 if o["dma"] else 1
+            last[name] = n
+            count[name] = count.get(name, 0) + step
+            where[n] = (name, count[name])
+            ins.then_inc(T.sem[name], step)
+
+
+def rank_program(g, core, T, topo):
+    rank = T.rank_of(core)
+    if rank is None:
+        return
+    cores = list(T.cores)
+    N = len(cores)
+    V, A, P, S = g.vector, g.scalar, g.tensor, g.sync
+    queues = {"g": g, "v": V, "a": A, "p": P, "s": S}
+    ops = []
+
+    def op(q, f, r=(), w=(), dma=False, cont=False, extra=()):
+        ops.append({"q": q, "f": f, "r": list(r), "w": list(w), "dma": dma, "cont": cont, "extra": list(extra)})
+
+    def fill(ap, c, key):
+        op("v", lambda: V.memset(ap, c), (), [key])
+
+    def ts(out, in0, s1, s2, op0, op1, r, w):
+        if op1 is None:
+            op("v", lambda: V.tensor_scalar(out, in0, s1, None, op0), r, w)
+        else:
+            op("v", lambda: V.tensor_scalar(out, in0, s1, s2, op0, op1), r, w)
+
+    def tt(out, in0, in1, alu, r, w):
+        op("v", lambda: V.tensor_tensor(out, in0, in1, alu), r, w)
+
+    def copy(out, in_, r, w):
+        op("v", lambda: V.tensor_copy(out, in_), r, w)
+
+    def act(out, in_, func, r, w, **kw):
+        op("a", lambda: A.activation(out, in_, func, **kw), r, w)
+
+    def quant(name, a, b, tile, r, w):
+        op("v", lambda: V.quantize_mx(T[name + "q"][:, a:b], T[name + "s"][:, a:b], tile), r, w)
+
+    def bank(key):
+        return (T.psa if key[0] == "A" else T.psb), 512 * int(key[1])
+
+    def ps(key, a, b):
+        buf, o = bank(key)
+        return buf[:, o + a:o + b]
+
+    def mm(key, wn, wa, xn, xa, n, start, stop, r, extra=()):
+        op("p", lambda: P.matmul_mx(ps(key, 0, n), T[wn + "q"][:, wa:wa + 128], T[wn + "s"][:, wa:wa + 128],
+                                    T[xn + "q"][:, xa:xa + n], T[xn + "s"][:, xa:xa + n], start, stop),
+           r, [key], cont=not start, extra=extra)
+
+    def dma(q, out, in_, r, w):
+        op(q, lambda: queues[q].dma_start(out, in_), r, w, dma=True)
+
+    def pick(dst, a, n, src, width, off, oa, r, w):
+        o = T[off][:, oa:oa + n // 16]
+        op("v", lambda: V.tensor_copy(T[dst + "q"][:, a:a + n].bitcast(dt.uint32),
+                                      T[src + "q"][:, 0:width].bitcast(dt.uint32).indirect(o)), r, [w + "q"])
+        op("a", lambda: A.activation(T[dst + "s"][:, a:a + n], T[src + "s"][:, 0:width].indirect(o), ACT.Copy), r, [w + "s"])
+
+    def slot(sender, receiver):
+        order = [o for o in cores if o != receiver]
+        if topo.chip(cores[-1]) == topo.chip(receiver) and cores[-1] in order:
+            order = order[-1:] + order[:-1]
+        return L * (len(order) - 1 - order.index(sender))
+
+    tw, hx, col = T.tw, T.hx, T.col
+    hxk = [["hx%d%d" % (h, b) for b in range(4)] for h in range(2)]
+    PW, S1, HOFF, HS, PW2R, PW2 = [col[:, 4 * k:4 * k + 1] for k in range(6)]
+
+    def spread_w(t):
+        for e in range(4):
+            a = 4 * (196 + 128 * t) + e
+            c = 4 * (68 + 8 * t + 6) + e
+            act(tw[:, a:a + 253:4], tw[:, 16:80], ACT.Identity, ["z0", "wp"], ["w6%d%d" % (t, e)], bias=tw[:, c:c + 1])
+
+    def quant_w6(t):
+        a = 4 * (196 + 128 * t)
+        quant("kw", 192 + 128 * t, 320 + 128 * t, tw[:, a:a + 512], ["w6%d%d" % (t, e) for e in range(4)] + ["z%d" % (t + 2)], ["kw%d" % (t + 1)])
+
+    def quant_state(t, h):
+        a, b = (0, PAD + H) if h == 0 else (PAD + H, PAD + TC)
+        quant("st%d" % t, a, b, hx[:, 4 * a:4 * b], hxk[h] + (["hxpad"] if h == 0 else []), ["st%d%d" % (t, h)])
+
+    dma("a", tw[:, 272:528], T.w[:, 0:256], [], ["wp"])
+    dma("s", hx[:, 8:8 + 4 * H], T.x[:, 0:4 * H], [], hxk[0])
+    dma("s", hx[:, 8 + 4 * H:8 + 8 * H], T.x[:, 4 * H:8 * H], [], hxk[1])
+    dma("s", T.zt[:], T.z[:], [], ["zt"])
+    op("g", lambda: g.iota(T.i16[:], [[0, 12], [-1, 16]], 16, 1), [], ["i16"])
+    op("g", lambda: g.iota(T.aip[:, 0:6], [[1, 6]], 0, 1), [], ["aip"])
+    op("g", lambda: g.iota(T.im[:], [[1, L]], 0, 0), [], ["im"])
+    op("g", lambda: g.iota(T.ipen[:], [[-16, 4]], 64, 1), [], ["ipen"])
+    aik = ["aik"]
+    op("v", lambda: V.memset(tw[:, 0:272], 0.0), [], ["z0", "it0", "it1", "it2a", "it2b"])
+    fill(tw[:, 528:784], 0.0, "z1")
+    fill(tw[:, 1040:1296], 0.0, "z2")
+    fill(hx[:, 0:8], 0.0, "hxpad")
+    op("v", lambda: V.memset(col[0:64, 8:9], 0.0), [], ["hoff0"])
+    op("v", lambda: V.memset(col[64:128, 8:9], float(H)), [], ["hoff1"])
+    ts(T.a16[:], T.i16[:], 15, None, ALU.bitwise_and, None, ["i16"], ["a16"])
+    ts(T.aik[:, 0:6], T.aip[:, 0:6], 63, None, ALU.bitwise_and, None, ["aip"], aik)
+    ts(T.m16[:], T.a16[:], 0.0, None, ALU.is_equal, None, ["a16"], ["m16"])
+    ts(T.f1[:, 0:5], T.aik[:, 0:5], 5.0, 1.0, ALU.is_lt, ALU.add, aik, ["f1"])
+    ts(S1, T.aik[:, 0:1], 6.0, 2.0 ** 23, ALU.is_lt, ALU.mult, aik, ["s1"])
+    op("v", lambda: V.tensor_reduce(PW, T.f1[:, 0:5], AxisListType.X, ALU.mult), ["f1"], ["pw"])
+    op("v", lambda: V.memset(T.cg[:], 0.0), [], ["cg0", "cg1", "cg2", "cg3", "cg4"])
+    ts(T.iv[:], T.im[:], PW, None, ALU.mult, None, ["im", "pw"], ["iv"])
+    fill(T.et[:], 0.0, "et")
+    ts(T.iv2[:], T.iv[:], 32, None, ALU.bitwise_and, None, ["iv"], ["iv2"])
+    fill(T.bt[:, 1:4 * H:4], BIT, "bt1")
+    fill(T.bt[:, 3:4 * H:4], 0.0, "bt3")
+    op("g", lambda: g.affine_select(T.et[:], T.et[:], [[-1, 520]], ALU.not_equal, 0.125, 4, 4), ["ipen"], ["et"])
+    act(T.bt[:, 2:4 * H:4], T.m16[:], ACT.Copy, ["m16"], ["bt2"], scale=BIT)
+    act(T.ci[:, 0:512:4], T.m16[:, 0:128], ACT.Copy, ["m16"], ["ci0"])
+    act(T.ci[:, 1:512:4], T.m16[:, 0:128], ACT.Copy, ["m16"], ["ci1"])
+    spread_w(0)
+    act(T.ci[:, 2:512:4], T.m16[:, 0:128], ACT.Identity, ["m16", "hoff0", "hoff1"], ["ci2"], scale=HOFF)
+    act(T.ci[:, 3:512:4], T.m16[:, 0:128], ACT.Copy, ["m16"], ["ci3"], scale=0.0)
+    fill(T.cg[32:48, 2:512:4], BIT, "cg4")
+    for h in range(2):
+        p0, p1, a = 64 * h, 64 * h + 64, 256 * h
+        ts(T.cg[p0:p1, a:a + 256:4], T.iv2[p0:p1, :], 16.0, col[p0:p1, 4:5], ALU.subtract, ALU.mult, ["iv2", "s1"], ["cg%d" % (2 * h)])
+        ts(T.cg[p0:p1, a + 1:a + 256:4], T.iv2[p0:p1, :], col[p0:p1, 4:5], -0.5, ALU.mult, ALU.mult, ["iv2", "s1"], ["cg%d" % (2 * h + 1)])
+    quant("kw", 0, 192, tw[:, 16:784], ["z0", "wp", "z1"], ["kw0"])
+    quant_w6(0)
+    fill(T.run[:, 0:PAD], FLOOR, "runpad")
+    fill(T.mc[:], MAGIC, "mc")
+    quant_state(0, 0)
+    quant("kcg", 0, 128, T.cg[:], ["cg0", "cg1", "cg2", "cg3", "cg4"], ["kcg"])
+    quant_state(0, 1)
+
+    eng = {c: engine_sets(c, cores, topo) for c in cores}
+    others = [o for o in cores if o != core]
+    early = topo.chip(cores[-1]) == topo.chip(core)
+    sent = 0
+    for t in range(R):
+        st, nxt, rep, land, val, sel = ["%s%d" % (s, k) for s, k in
+                                        (("st", t), ("st", t + 1), ("rep", t), ("land", t), ("val", t), ("sel", t))]
+        ofr, ofl = "ofr%d" % t, "ofl%d" % t
+        kwp = ["kw0", "kw1"] if t else ["kw0"]
+        kws = ["kw%d" % t, "kw%d" % (t + 1)]
+        mm("A0", "kw", 64 + 8 * t, st, PAD, H, True, False, kwp + [st + "0"])
+        mm("A1", "kw", 192 + 128 * t, st, PAD, H, True, False, kws + [st + "0"])
+        mm("A0", "kw", 8 * t, st, PAD + H, H, False, True, kwp + [st + "1"])
+        mm("A1", "kw", 128 + 128 * t, st, PAD + H, H, False, True, kws + [st + "1"])
+        if t == 0:
+            ts(T.apen[:], T.ipen[:], 48, None, ALU.bitwise_and, None, ["ipen"], ["apen"])
+        ts(T.bt[:, 0:4 * H:4], ps("A0", 0, H), 0.0, BIT, ALU.is_lt, ALU.mult, [], ["A0", "bt0"])
+        act(T.sp[:], ps("A1", 0, H), ACT.Copy, [], ["A1", "sp"], scale=2.0 ** -20)
+        quant("kb", 0, H, T.bt[:], ["bt0", "bt1", "bt2", "bt3"], ["kb"])
+        mm("A2", "kcg", 0, "kb", 0, H, True, True, ["kcg", "kb"])
+        if t == 0:
+            ts(T.pen[:], T.apen[:], 0.0, -2.0 ** 60, ALU.not_equal, ALU.mult, ["apen"], ["pen"])
+            quant("kci", 0, 128, T.ci[:], ["ci0", "ci1", "ci2", "ci3"], ["kci"])
+        tt(T.key[:], ps("A2", 0, H), T.sp[:], ALU.min, ["sp"], ["A2", "key"])
+        op("v", lambda: V.tensor_tensor_scan(T.run[:, PAD:], T.key[:], T.key[:], FLOOR, ALU.max, ALU.max), ["key"], ["run"])
+        top = PAD + H - 1
+        act(T.junk[:], T.run[:], ACT.Sign, ["run", "runpad"], ["junk", "cnt"], bias=T.run[:, top:top + 1], scale=-1.0,
+            accum_out=T.cnt[:, 0:1])
+        ts(tw[0:64, 2:16:4], T.pen[0:64, :], T.run[0:64, top:top + 1], T.run[64:128, top:top + 1], ALU.add, ALU.is_ge,
+           ["pen", "run"], ["it2a"])
+        ts(tw[64:128, 2:16:4], T.pen[64:128, :], T.run[64:128, top:top + 1], T.run[0:64, top:top + 1], ALU.add, ALU.is_gt,
+           ["pen", "run"], ["it2b"])
+        ts(T.cnt[:, 4:5], T.cnt[:, 0:1], MAGIC, MAGIC, ALU.add, ALU.subtract, ["cnt"], ["hi"])
+        ts(tw[:, 0:16:4], T.mc[:], T.cnt[:, 0:1], MAGIC, ALU.add, ALU.subtract, ["mc", "cnt"], ["it0"])
+        ts(tw[:, 1:16:4], tw[:, 2:16:4], T.cnt[:, 0:1], T.cnt[:, 4:5], ALU.mult, ALU.subtract, ["cnt", "hi", "it2a", "it2b"], ["it1"])
+        quant("ki", 0, 128, tw[:, 0:512], ["it0", "it1", "it2a", "it2b", "z0", "wp"], ["ki"])
+        mm("A3", "kci", 0, "ki", 0, 128, True, True, ["kci", "ki"])
+        copy(T[ofr][:], ps("A3", 0, 4), [], ["A3", ofr])
+        pick(rep, 0, L, st, TC + PAD, ofr, 0, [st + "0", st + "1", ofr], rep)
+        for kind in "qs":
+            trs = []
+            for c in others:
+                pos = slot(core, c)
+                rid, pid, _ = topo.addr(c)
+                mask = sum(1 << e for e in eng[core][c])
+                src, dst = T[rep + kind][:, 0:L], T[land + kind][:, pos:pos + L]
+                if kind == "q":
+                    src, dst = src.bitcast(dt.uint8), dst.bitcast(dt.uint8)
+                trs.append(RemoteDMATransfer(dst_ids=[DstId(rid=rid, pnc=pid)], dma_engine_mask=mask,
+                                             remote_sem=T.sem["arr%d_%d" % (t, rank)], src=src, dst=dst))
+                sent += len(eng[core][c])
+            op("g", lambda trs=trs: g.remote_dma_fused(trs, local_sem=T.sem.sent), [rep + kind], [], dma=True)
+        if t == 0:
+            op("v", lambda: V.memset(T.cl[:], 0.0), [], ["cl0", "cl2"])
+            ts(T.f2[:, 0:5], T.aik[:, 0:5], 5.0, 1.0, ALU.is_ge, ALU.add, aik, ["f2"])
+            op("v", lambda: V.memset(col[0:64, 12:13], 2.0 ** -49), [], ["hs0"])
+            op("v", lambda: V.memset(col[64:128, 12:13], 2.0 ** -43), [], ["hs1"])
+            op("v", lambda: V.tensor_reduce(PW2R, T.f2[:, 0:5], AxisListType.X, ALU.mult), ["f2"], ["pw2r"])
+            act(T.cl[32:48, 2:512:4], T.m16[32:48, 0:128], ACT.Identity, ["m16"], ["cl2"], scale=2.0 ** -14, bias=-2.0 ** -14)
+            fill(T.d0[:], 1.0, "d0")
+            ts(PW2, PW2R, S1, HS, ALU.mult, ALU.mult, ["pw2r", "s1", "hs0", "hs1"], ["pw2"])
+            act(T.cl[:, 0:512:4], T.m16[:, 0:128], ACT.Identity, ["m16", "pw2"], ["cl0"], scale=0.0, bias=PW2)
+            act(T.et2[:], T.et[:], ACT.Copy, ["et"], ["et2"], scale=-0.5)
+            for b in range(2):
+                quant("ke", 128 * b, 128 * b + 128, T.et[:, 4 - b:516 - b], ["et"], ["ke%d" % b])
+            fill(T.d0[:, 0:H:16], 0.0, "d0")
+            quant("kcl", 0, 128, T.cl[:], ["cl0", "cl2"], ["kcl"])
+            for b in range(2, 4):
+                quant("ke", 128 * b, 128 * b + 128, T.et[:, 4 - b:516 - b], ["et"], ["ke%d" % b])
+        mm("B3", "kcl", 0, "kb", 0, H, True, True, ["kcl", "kb"])
+        quant(land, 192, 320, T.bt[:, 0:512], ["bt0", "bt1", "bt2", "bt3"], [land + "pad"])
+        op("v", lambda: V.tensor_tensor_scan(T.ls[:], T.d0[:], ps("B3", 0, H), 0.0, ALU.mult, ALU.max), ["d0"], ["B3", "ls"])
+        quant(rep, 64, 192, T.bt[:, 0:512], ["bt0", "bt1", "bt2", "bt3"], [rep + "pad"])
+        for b in range(4):
+            mm("A%d" % b, "ke", 128 * b, st, PAD, H, True, False, ["ke%d" % b, st + "0"])
+        copy(T.lc[:], T.ls[:, 15:H:16], ["ls"], ["lc"])
+        if t == 0:
+            fill(T.vt[:, 256:512], 0.0, "vtpad")
+            fill(T.lf[0:32, 24:32], 0.0, "lfpad")
+        ts(T.li[:, 0:12], T.lc[:], 63, None, ALU.bitwise_and, None, ["lc"], ["li0"])
+        ts(T.li[:, 12:24], T.lc[:], 6, None, ALU.logical_shift_right, None, ["lc"], ["li1"])
+        if t < R - 1:
+            a = 4 * (196 + 128 * (t + 1) + 64)
+            fill(tw[:, a:a + 256], 0.0, "z%d" % (t + 3))
+            spread_w(t + 1)
+        copy(T[ofl][:], T.li[:], ["li0", "li1"], [ofl])
+        copy(T.lf[0:32, 0:24], T.li[0:32, :], ["li0", "li1"], ["lf"])
+        if t == 0:
+            for b in range(4):
+                quant("kf", 128 * b, 128 * b + 128, T.et2[:, 4 - b:516 - b], ["et2"], ["kf%d" % b])
+        op("v", lambda: V.transpose(T.lt[0:32, :], T.lf[0:32, :]), ["lf", "lfpad"], ["lt"])
+        dma("s", T.lv[t], T.lt[0:24, 0:16], ["lt"], ["lv%d" % t])
+        if t < R - 1:
+            quant_w6(t + 1)
+        if t == 1:
+            quant("kz", 0, 128, T.zt[:], ["zt"], ["kz"])
+
+        def unpack(r, start, stop):
+            c = cores[r]
+            for b in range(4):
+                if c == core:
+                    mm("B%d" % b, "ke", 128 * b, rep, 0, 128, start, stop, ["ke%d" % b, rep + "q", rep + "s", rep + "pad"])
+                else:
+                    extra = [("arr%d_%d" % (t, r), 2 * len(eng[c][core]))] if b == 0 else []
+                    mm("B%d" % b, "ke", 128 * b, land, slot(c, core), 128, start, stop, ["ke%d" % b, land + "pad"], extra)
+
+        if early:
+            unpack(N - 1, True, True)
+            for b in range(4):
+                act(T.dl[:, L * b:L * b + L], ps("B%d" % b, 0, L), ACT.Copy, [], ["B%d" % b, "dl%d" % b])
+            for r in range(N - 1):
+                unpack(r, r == 0, r == N - 2)
+            for b in range(4):
+                tt(T.vt[:, b:256:4], ps("B%d" % b, 0, L), T.dl[:, L * b:L * b + L], ALU.add, ["dl%d" % b], ["B%d" % b, "vt%d" % b])
+        else:
+            for r in range(N):
+                unpack(r, r == 0, r == N - 1)
+            for b in range(4):
+                if b % 2 == 0:
+                    act(T.vt[:, b:256:4], ps("B%d" % b, 0, L), ACT.Copy, [], ["B%d" % b, "vt%d" % b])
+                else:
+                    copy(T.vt[:, b:256:4], ps("B%d" % b, 0, L), [], ["B%d" % b, "vt%d" % b])
+        quant(val, 0, 128, T.vt[:], ["vt0", "vt1", "vt2", "vt3", "vtpad"], [val])
+        for b in range(4):
+            mm("B%d" % b, "ke", 128 * b, st, PAD + H, H, True, False, ["ke%d" % b, st + "1"])
+        for h in range(2):
+            pick(sel, H * h, H, val, L, ofl, 12 * h, [val, ofl], sel + str(h))
+        for h in range(2):
+            for b in range(4):
+                mm("AB"[h] + str(b), "kf", 128 * b, sel, H * h, H, False, True, ["kf%d" % b, sel + str(h) + "q", sel + str(h) + "s"])
+
+        def drain(h, b, q):
+            a = 4 * (PAD + H * h) + b
+            k = "AB"[h] + str(b)
+            if q == "a":
+                act(hx[:, a:a + 4 * H - 3:4], ps(k, 0, H), ACT.Copy, [], [k, hxk[h][b]], scale=8.0)
+            else:
+                ts(hx[:, a:a + 4 * H - 3:4], ps(k, 0, H), 8.0, None, ALU.mult, None, [], [k, hxk[h][b]])
+
+        for b in range(4):
+            drain(0, b, "va"[b % 2])
+        quant_state(t + 1, 0)
+        drain(1, 0, "a")
+        drain(1, 1, "a")
+        drain(1, 2, "v")
+        drain(1, 3, "a")
+        if t == R - 1:
+            dma("s", T.oc[:, 0:4 * H], T[nxt + "q"][:, PAD:PAD + H].bitcast(dt.uint8), [nxt + "0"], ["oc0"])
+            mm("A0", "kz", 0, nxt, PAD, H, True, True, ["kz", nxt + "0"])
+            act(T.ysb[:, 0:H], ps("A0", 0, H), ACT.Copy, [], ["A0", "y0"])
+            dma("a", T.y[:, 0:H], T.ysb[:, 0:H], ["y0"], ["oy0"])
+        quant_state(t + 1, 1)
+
+    fin = "st%d" % R
+    mm("A1", "kz", 0, fin, PAD + H, H, True, True, ["kz", fin + "1"])
+    dma("s", T.oc[:, 4 * H:8 * H], T[fin + "q"][:, PAD + H:PAD + TC].bitcast(dt.uint8), [fin + "1"], ["oc1"])
+    copy(T.ysb[:, H:TC], ps("A1", 0, H), [], ["A1", "y1"])
+    for k in range(2):
+        dma("a", T.osc[4 * k:4 * k + 4, :], T[fin + "s"][32 * k:32 * k + 4, PAD:PAD + TC], [fin + "0", fin + "1"], ["os%d" % k])
+    dma("s", T.y[:, H:TC], T.ysb[:, H:TC], ["y1"], ["oy1"])
+    for k in range(2, 4):
+        dma("a", T.osc[4 * k:4 * k + 4, :], T[fin + "s"][32 * k:32 * k + 4, PAD:PAD + TC], [fin + "0", fin + "1"], ["os%d" % k])
+    op("g", None, extra=[("sent", sent)], dma=True)
+    op("a", None, ["oy0", "os0", "os1", "os2", "os3"], dma=True)
+    op("s", None, ["oc0", "oc1", "oy1", "lv0", "lv1", "lv2"], dma=True)
+    emit_program(ops, queues, T)

@@ -11,17 +11,17 @@ SCRATCH = {
     "tw": ("sbuf", [128, 4 * 580], BF), "hx": ("sbuf", [128, 4 * (TC + PAD)], BF),
     "bt": ("sbuf", [128, 4 * H], BF), "cg": ("sbuf", [128, 512], BF), "ci": ("sbuf", [128, 512], BF),
     "cl": ("sbuf", [128, 512], BF), "et": ("sbuf", [128, 520], BF), "et2": ("sbuf", [128, 520], BF),
-    "vt": ("sbuf", [128, 512], BF), "zt": ("sbuf", [128, 512], BF), "m16": ("sbuf", [128, H], BF),
-    "junk": ("sbuf", [128, H + PAD], BF),
+    "vt": ("sbuf", [128, 512], BF), "zt": ("sbuf", [128, 512], BF), "jm": ("sbuf", [128, H], BF),
+    "etr": ("sbuf", [128, 520], BF), "low": ("sbuf", [128, H], BF), "junk": ("sbuf", [128, H + PAD], BF),
+    "d0": ("sbuf", [128, H], BF),
     "aip": ("sbuf", [128, 8], I32), "aik": ("sbuf", [128, 8], I32), "im": ("sbuf", [128, L], I32),
-    "iv": ("sbuf", [128, L], I32),
-    "iv2": ("sbuf", [128, L], I32), "i16": ("sbuf", [128, H], I32), "a16": ("sbuf", [128, H], I32),
+    "iv": ("sbuf", [128, L], I32), "iv2": ("sbuf", [128, L], I32),
     "ipen": ("sbuf", [128, 4], I32), "apen": ("sbuf", [128, 4], I32), "lc": ("sbuf", [128, 12], I32),
     "li": ("sbuf", [128, 24], I32),
     "f1": ("sbuf", [128, 8], F32), "f2": ("sbuf", [128, 8], F32), "col": ("sbuf", [128, 32], F32),
-    "pen": ("sbuf", [128, 4], F32), "mc": ("sbuf", [128, 4], F32), "sp": ("sbuf", [128, H], F32),
-    "key": ("sbuf", [128, H], F32), "run": ("sbuf", [128, H + PAD], F32), "cnt": ("sbuf", [128, 8], F32),
-    "d0": ("sbuf", [128, H], F32), "ls": ("sbuf", [128, H], F32), "lf": ("sbuf", [128, 32], F32),
+    "pen": ("sbuf", [128, 4], F32), "mc": ("sbuf", [128, 4], F32), "pc": ("sbuf", [128, 4], F32),
+    "run": ("sbuf", [128, H + PAD], F32), "cnt": ("sbuf", [128, 8], F32),
+    "ls": ("sbuf", [128, H], F32), "lf": ("sbuf", [128, 32], F32),
     "lt": ("sbuf", [128, 32], F32), "ysb": ("sbuf", [128, TC], F32), "dl": ("sbuf", [128, 4 * L], F32),
 }
 
@@ -48,8 +48,10 @@ SEMAPHORES = (["c%d" % k for k in range(NC)] + ["d%d" % k for k in range(ND)]
               + ["arr%d_%d" % (t, r) for t in range(R) for r in range(4)] + ["sent"])
 
 BIT = 2.0 ** 26
-FLOOR = -2.0 ** 51
+FLOOR = -2.0 ** 70
 MAGIC = 1.5 * 2.0 ** 27
+CUT = (192, 192, 192, 192)
+DRAIN = "vavavava"
 
 
 def engine_sets(src, cores, topo):
@@ -137,8 +139,14 @@ def rank_program(g, core, T, topo):
     def op(q, f, r=(), w=(), dma=False, cont=False, extra=()):
         ops.append({"q": q, "f": f, "r": list(r), "w": list(w), "dma": dma, "cont": cont, "extra": list(extra)})
 
-    def fill(ap, c, key):
-        op("v", lambda: V.memset(ap, c), (), [key])
+    def fill(ap, c, *keys):
+        op("v", lambda: V.memset(ap, c), (), keys)
+
+    def iota(ap, pattern, base, step, w, whole=False):
+        if whole:
+            op("g", lambda: g.iota(ap, pattern, base, step), [], w)
+        else:
+            op("g", lambda: g.iota(ap, pattern, base, step, allow_small_or_imprecise_dtypes=True), [], w)
 
     def ts(out, in0, s1, s2, op0, op1, r, w):
         if op1 is None:
@@ -187,7 +195,7 @@ def rank_program(g, core, T, topo):
 
     tw, hx, col = T.tw, T.hx, T.col
     hxk = [["hx%d%d" % (h, b) for b in range(4)] for h in range(2)]
-    PW, S1, HOFF, HS, PW2R, PW2 = [col[:, 4 * k:4 * k + 1] for k in range(6)]
+    PW, S1, R32, HS, PW2R, PW2 = [col[:, 4 * k:4 * k + 1] for k in range(6)]
 
     def spread_w(t):
         for e in range(4):
@@ -199,82 +207,95 @@ def rank_program(g, core, T, topo):
         a = 4 * (196 + 128 * t)
         quant("kw", 192 + 128 * t, 320 + 128 * t, tw[:, a:a + 512], ["w6%d%d" % (t, e) for e in range(4)] + ["z%d" % (t + 2)], ["kw%d" % (t + 1)])
 
+    def zeros_w6(t):
+        a = 4 * (196 + 128 * t + 64)
+        act(tw[:, a:a + 256], tw[:, 16:272], ACT.Copy, ["z0"], ["z%d" % (t + 2)])
+
     def quant_state(t, h):
-        a, b = (0, PAD + H) if h == 0 else (PAD + H, PAD + TC)
+        a, b = (0, PAD + CUT[t]) if h == 0 else (PAD + CUT[t], PAD + TC)
         quant("st%d" % t, a, b, hx[:, 4 * a:4 * b], hxk[h] + (["hxpad"] if h == 0 else []), ["st%d%d" % (t, h)])
 
     dma("a", tw[:, 272:528], T.w[:, 0:256], [], ["wp"])
-    dma("s", hx[:, 8:8 + 4 * H], T.x[:, 0:4 * H], [], hxk[0])
-    dma("s", hx[:, 8 + 4 * H:8 + 8 * H], T.x[:, 4 * H:8 * H], [], hxk[1])
-    dma("s", T.zt[:], T.z[:], [], ["zt"])
-    op("g", lambda: g.iota(T.i16[:], [[0, 12], [-1, 16]], 16, 1), [], ["i16"])
-    op("g", lambda: g.iota(T.aip[:, 0:6], [[1, 6]], 0, 1), [], ["aip"])
-    op("g", lambda: g.iota(T.im[:], [[1, L]], 0, 0), [], ["im"])
-    op("g", lambda: g.iota(T.ipen[:], [[-16, 4]], 64, 1), [], ["ipen"])
+    dma("s", hx[:, 8:8 + 4 * CUT[0]], T.x[:, 0:4 * CUT[0]], [], hxk[0])
+    dma("s", hx[:, 8 + 4 * CUT[0]:8 + 4 * TC], T.x[:, 4 * CUT[0]:4 * TC], [], hxk[1])
+    iota(T.aip[:, 0:6], [[1, 6]], 0, 1, ["aip"], True)
+    iota(T.pc[:, 0:2], [[0, 2]], -15, 2, ["pc"])
+    iota(T.im[:], [[1, L]], 0, 0, ["im"], True)
+    iota(T.jm[:], [[0, 12], [-2, 16]], 0, 2, ["jm"])
+    iota(T.cg[:], [[0, 512]], 0, 0, ["cg0", "cg1", "cg2", "cg3"])
+    iota(T.ipen[:], [[-16, 4]], 64, 1, ["ipen"], True)
+    iota(T.etr[:], [[-1, 520]], 4, 4, ["etr"])
+    iota(T.d0[:], [[0, 12], [1, 16]], 0, 0, ["d0r"])
     aik = ["aik"]
-    op("v", lambda: V.memset(tw[:, 0:272], 0.0), [], ["z0", "it0", "it1", "it2a", "it2b"])
+    fill(tw[:, 0:272], 0.0, "z0", "it0", "it1", "it2a", "it2b")
     fill(tw[:, 528:784], 0.0, "z1")
-    fill(tw[:, 1040:1296], 0.0, "z2")
-    fill(hx[:, 0:8], 0.0, "hxpad")
-    op("v", lambda: V.memset(col[0:64, 8:9], 0.0), [], ["hoff0"])
-    op("v", lambda: V.memset(col[64:128, 8:9], float(H)), [], ["hoff1"])
-    ts(T.a16[:], T.i16[:], 15, None, ALU.bitwise_and, None, ["i16"], ["a16"])
     ts(T.aik[:, 0:6], T.aip[:, 0:6], 63, None, ALU.bitwise_and, None, ["aip"], aik)
-    ts(T.m16[:], T.a16[:], 0.0, None, ALU.is_equal, None, ["a16"], ["m16"])
+    zeros_w6(0)
+    act(T.vt[:, 256:512], tw[:, 16:272], ACT.Copy, ["z0"], ["vtpad"])
+    ts(R32, T.pc[:, 0:1], 2 * MAGIC, 2 * MAGIC, ALU.add, ALU.subtract, ["pc"], ["r32"])
     ts(T.f1[:, 0:5], T.aik[:, 0:5], 5.0, 1.0, ALU.is_lt, ALU.add, aik, ["f1"])
-    ts(S1, T.aik[:, 0:1], 6.0, 2.0 ** 23, ALU.is_lt, ALU.mult, aik, ["s1"])
+    ts(S1, T.aik[:, 0:1], 6.0, 2.0 ** 42, ALU.is_lt, ALU.mult, aik, ["s1"])
     op("v", lambda: V.tensor_reduce(PW, T.f1[:, 0:5], AxisListType.X, ALU.mult), ["f1"], ["pw"])
-    op("v", lambda: V.memset(T.cg[:], 0.0), [], ["cg0", "cg1", "cg2", "cg3", "cg4"])
+    ts(T.f2[:, 0:5], T.aik[:, 0:5], 5.0, 1.0, ALU.is_ge, ALU.add, aik, ["f2"])
     ts(T.iv[:], T.im[:], PW, None, ALU.mult, None, ["im", "pw"], ["iv"])
-    fill(T.et[:], 0.0, "et")
+    fill(T.bt[:, 1:4 * H:2], BIT, "bt1")
     ts(T.iv2[:], T.iv[:], 32, None, ALU.bitwise_and, None, ["iv"], ["iv2"])
-    fill(T.bt[:, 1:4 * H:4], BIT, "bt1")
-    fill(T.bt[:, 3:4 * H:4], 0.0, "bt3")
-    op("g", lambda: g.affine_select(T.et[:], T.et[:], [[-1, 520]], ALU.not_equal, 0.125, 4, 4), ["ipen"], ["et"])
-    act(T.bt[:, 2:4 * H:4], T.m16[:], ACT.Copy, ["m16"], ["bt2"], scale=BIT)
-    act(T.ci[:, 0:512:4], T.m16[:, 0:128], ACT.Copy, ["m16"], ["ci0"])
-    act(T.ci[:, 1:512:4], T.m16[:, 0:128], ACT.Copy, ["m16"], ["ci1"])
+    ts(T.bt[:, 2:4 * H:4], T.jm[:], R32, BIT, ALU.is_equal, ALU.mult, ["jm", "r32"], ["bt2"])
+    fill(hx[:, 0:8], 0.0, "hxpad")
+    op("v", lambda: V.tensor_reduce(PW2R, T.f2[:, 0:5], AxisListType.X, ALU.mult), ["f2"], ["pw2r"])
     spread_w(0)
-    act(T.ci[:, 2:512:4], T.m16[:, 0:128], ACT.Identity, ["m16", "hoff0", "hoff1"], ["ci2"], scale=HOFF)
-    act(T.ci[:, 3:512:4], T.m16[:, 0:128], ACT.Copy, ["m16"], ["ci3"], scale=0.0)
-    fill(T.cg[32:48, 2:512:4], BIT, "cg4")
+    for e in (0, 1, 3):
+        act(T.ci[:, e:512:4], T.bt[:, 2:512:4], ACT.Copy, ["bt2"], ["ci%d" % e], scale=1 / BIT)
     for h in range(2):
+        act(T.ci[64 * h:64 * h + 64, 2:512:4], T.bt[64 * h:64 * h + 64, 2:512:4], ACT.Copy, ["bt2"], ["ci2%d" % h], scale=h * H / BIT)
+    quant("kw", 0, 192, tw[:, 16:784], ["z0", "wp", "z1"], ["kw0"])
+    fill(T.low[:], FLOOR, "low")
+    fill(T.run[:, 0:PAD], FLOOR, "runpad")
+    quant_w6(0)
+
+    def member(h):
         p0, p1, a = 64 * h, 64 * h + 64, 256 * h
         ts(T.cg[p0:p1, a:a + 256:4], T.iv2[p0:p1, :], 16.0, col[p0:p1, 4:5], ALU.subtract, ALU.mult, ["iv2", "s1"], ["cg%d" % (2 * h)])
         ts(T.cg[p0:p1, a + 1:a + 256:4], T.iv2[p0:p1, :], col[p0:p1, 4:5], -0.5, ALU.mult, ALU.mult, ["iv2", "s1"], ["cg%d" % (2 * h + 1)])
-    quant("kw", 0, 192, tw[:, 16:784], ["z0", "wp", "z1"], ["kw0"])
-    quant_w6(0)
-    fill(T.run[:, 0:PAD], FLOOR, "runpad")
-    fill(T.mc[:], MAGIC, "mc")
+
+    member(0)
     quant_state(0, 0)
-    quant("kcg", 0, 128, T.cg[:], ["cg0", "cg1", "cg2", "cg3", "cg4"], ["kcg"])
+    member(1)
     quant_state(0, 1)
+    dma("s", T.zt[:], T.z[:], ["st01"], ["zt"])
+    act(T.et2[:], T.etr[:], ACT.Abs, ["etr"], ["et2"])
+    act(T.et[:], T.et2[:], ACT.Relu, ["et2"], ["et"], scale=-0.125, bias=0.125)
 
     eng = {c: engine_sets(c, cores, topo) for c in cores}
     others = [o for o in cores if o != core]
     early = topo.chip(cores[-1]) == topo.chip(core)
     sent = 0
+    bts = ["bt0", "bt1", "bt2"]
     for t in range(R):
         st, nxt, rep, land, val, sel = ["%s%d" % (s, k) for s, k in
                                         (("st", t), ("st", t + 1), ("rep", t), ("land", t), ("val", t), ("sel", t))]
         ofr, ofl = "ofr%d" % t, "ofl%d" % t
+        C = CUT[t + 1]
+        span = ((0, C), (C, TC - C))
+        both = [st + "0", st + "1"]
         kwp = ["kw0", "kw1"] if t else ["kw0"]
         kws = ["kw%d" % t, "kw%d" % (t + 1)]
         mm("A0", "kw", 64 + 8 * t, st, PAD, H, True, False, kwp + [st + "0"])
-        mm("A1", "kw", 192 + 128 * t, st, PAD, H, True, False, kws + [st + "0"])
-        mm("A0", "kw", 8 * t, st, PAD + H, H, False, True, kwp + [st + "1"])
-        mm("A1", "kw", 128 + 128 * t, st, PAD + H, H, False, True, kws + [st + "1"])
+        mm("A0", "kw", 8 * t, st, PAD + H, H, False, True, kwp + both)
+        mm("A1", "kw", 192 + 128 * t, st, PAD, H, True, False, kws + both)
+        mm("A1", "kw", 128 + 128 * t, st, PAD + H, H, False, False, kws + both)
         if t == 0:
+            quant("kcg", 0, 128, T.cg[:], ["cg0", "cg1", "cg2", "cg3"], ["kcg"])
             ts(T.apen[:], T.ipen[:], 48, None, ALU.bitwise_and, None, ["ipen"], ["apen"])
         ts(T.bt[:, 0:4 * H:4], ps("A0", 0, H), 0.0, BIT, ALU.is_lt, ALU.mult, [], ["A0", "bt0"])
-        act(T.sp[:], ps("A1", 0, H), ACT.Copy, [], ["A1", "sp"], scale=2.0 ** -20)
-        quant("kb", 0, H, T.bt[:], ["bt0", "bt1", "bt2", "bt3"], ["kb"])
-        mm("A2", "kcg", 0, "kb", 0, H, True, True, ["kcg", "kb"])
+        quant("kb", 0, H, T.bt[:], bts, ["kb"])
+        mm("A1", "kcg", 0, "kb", 0, H, False, True, ["kcg", "kb"])
         if t == 0:
-            ts(T.pen[:], T.apen[:], 0.0, -2.0 ** 60, ALU.not_equal, ALU.mult, ["apen"], ["pen"])
-            quant("kci", 0, 128, T.ci[:], ["ci0", "ci1", "ci2", "ci3"], ["kci"])
-        tt(T.key[:], ps("A2", 0, H), T.sp[:], ALU.min, ["sp"], ["A2", "key"])
-        op("v", lambda: V.tensor_tensor_scan(T.run[:, PAD:], T.key[:], T.key[:], FLOOR, ALU.max, ALU.max), ["key"], ["run"])
+            ts(T.pen[:], T.apen[:], 0.0, -2.0 ** 80, ALU.not_equal, ALU.mult, ["apen"], ["pen"])
+            quant("kci", 0, 128, T.ci[:], ["ci0", "ci1", "ci20", "ci21", "ci3"], ["kci"])
+        op("v", lambda: V.tensor_tensor_scan(T.run[:, PAD:], ps("A1", 0, H), T.low[:], FLOOR, ALU.max, ALU.max), ["low"], ["A1", "run"])
+        if t == 0:
+            fill(T.mc[:], MAGIC, "mc")
         top = PAD + H - 1
         act(T.junk[:], T.run[:], ACT.Sign, ["run", "runpad"], ["junk", "cnt"], bias=T.run[:, top:top + 1], scale=-1.0,
             accum_out=T.cnt[:, 0:1])
@@ -287,8 +308,10 @@ def rank_program(g, core, T, topo):
         ts(tw[:, 1:16:4], tw[:, 2:16:4], T.cnt[:, 0:1], T.cnt[:, 4:5], ALU.mult, ALU.subtract, ["cnt", "hi", "it2a", "it2b"], ["it1"])
         quant("ki", 0, 128, tw[:, 0:512], ["it0", "it1", "it2a", "it2b", "z0", "wp"], ["ki"])
         mm("A3", "kci", 0, "ki", 0, 128, True, True, ["kci", "ki"])
+        if t == 0:
+            quant("ke", 0, 128, T.et[:, 4:516], ["et"], ["ke0"])
         copy(T[ofr][:], ps("A3", 0, 4), [], ["A3", ofr])
-        pick(rep, 0, L, st, TC + PAD, ofr, 0, [st + "0", st + "1", ofr], rep)
+        pick(rep, 0, L, st, TC + PAD, ofr, 0, both + [ofr], rep)
         for kind in "qs":
             trs = []
             for c in others:
@@ -303,113 +326,116 @@ def rank_program(g, core, T, topo):
                 sent += len(eng[core][c])
             op("g", lambda trs=trs: g.remote_dma_fused(trs, local_sem=T.sem.sent), [rep + kind], [], dma=True)
         if t == 0:
-            op("v", lambda: V.memset(T.cl[:], 0.0), [], ["cl0", "cl2"])
-            ts(T.f2[:, 0:5], T.aik[:, 0:5], 5.0, 1.0, ALU.is_ge, ALU.add, aik, ["f2"])
-            op("v", lambda: V.memset(col[0:64, 12:13], 2.0 ** -49), [], ["hs0"])
-            op("v", lambda: V.memset(col[64:128, 12:13], 2.0 ** -43), [], ["hs1"])
-            op("v", lambda: V.tensor_reduce(PW2R, T.f2[:, 0:5], AxisListType.X, ALU.mult), ["f2"], ["pw2r"])
-            act(T.cl[32:48, 2:512:4], T.m16[32:48, 0:128], ACT.Identity, ["m16"], ["cl2"], scale=2.0 ** -14, bias=-2.0 ** -14)
-            fill(T.d0[:], 1.0, "d0")
-            ts(PW2, PW2R, S1, HS, ALU.mult, ALU.mult, ["pw2r", "s1", "hs0", "hs1"], ["pw2"])
-            act(T.cl[:, 0:512:4], T.m16[:, 0:128], ACT.Identity, ["m16", "pw2"], ["cl0"], scale=0.0, bias=PW2)
+            fill(T.cl[:], 0.0, "cl0", "cl2")
+            for h in range(2):
+                ts(col[64 * h:64 * h + 64, 20:21], col[64 * h:64 * h + 64, 16:17], col[64 * h:64 * h + 64, 4:5], 2.0 ** (6 * h - 68),
+                   ALU.mult, ALU.mult, ["pw2r", "s1"], ["pw2%d" % h])
             act(T.et2[:], T.et[:], ACT.Copy, ["et"], ["et2"], scale=-0.5)
-            for b in range(2):
+            act(T.cl[32:48, 2:512:4], T.ci[32:48, 0:512:4], ACT.Identity, ["ci0"], ["cl2"], scale=2.0 ** -14, bias=-2.0 ** -14)
+            act(T.cl[:, 0:512:4], T.ci[:, 0:512:4], ACT.Identity, ["ci0", "pw20", "pw21"], ["cl0"], scale=0.0, bias=PW2)
+            act(T.d0[:], T.d0[:], ACT.Sign, ["d0r"], ["d0"])
+            for b in range(1, 4):
                 quant("ke", 128 * b, 128 * b + 128, T.et[:, 4 - b:516 - b], ["et"], ["ke%d" % b])
-            fill(T.d0[:, 0:H:16], 0.0, "d0")
+        quant(land, 192, 320, T.bt[:, 0:512], bts, [land + "pad"])
+        quant(rep, 64, 192, T.bt[:, 0:512], bts, [rep + "pad"])
+        if t == 0:
             quant("kcl", 0, 128, T.cl[:], ["cl0", "cl2"], ["kcl"])
-            for b in range(2, 4):
-                quant("ke", 128 * b, 128 * b + 128, T.et[:, 4 - b:516 - b], ["et"], ["ke%d" % b])
-        mm("B3", "kcl", 0, "kb", 0, H, True, True, ["kcl", "kb"])
-        quant(land, 192, 320, T.bt[:, 0:512], ["bt0", "bt1", "bt2", "bt3"], [land + "pad"])
-        op("v", lambda: V.tensor_tensor_scan(T.ls[:], T.d0[:], ps("B3", 0, H), 0.0, ALU.mult, ALU.max), ["d0"], ["B3", "ls"])
-        quant(rep, 64, 192, T.bt[:, 0:512], ["bt0", "bt1", "bt2", "bt3"], [rep + "pad"])
-        for b in range(4):
-            mm("A%d" % b, "ke", 128 * b, st, PAD, H, True, False, ["ke%d" % b, st + "0"])
+        mm("A2", "kcl", 0, "kb", 0, H, True, True, ["kcl", "kb"])
+        op("v", lambda: V.tensor_tensor_scan(T.ls[:], T.d0[:], ps("A2", 0, H), 0.0, ALU.mult, ALU.max), ["d0"], ["A2", "ls"])
+        if t == 0:
+            for b in range(2):
+                quant("kf", 128 * b, 128 * b + 128, T.et2[:, 4 - b:516 - b], ["et2"], ["kf%d" % b])
         copy(T.lc[:], T.ls[:, 15:H:16], ["ls"], ["lc"])
         if t == 0:
-            fill(T.vt[:, 256:512], 0.0, "vtpad")
-            fill(T.lf[0:32, 24:32], 0.0, "lfpad")
+            quant("kf", 256, 384, T.et2[:, 2:514], ["et2"], ["kf2"])
         ts(T.li[:, 0:12], T.lc[:], 63, None, ALU.bitwise_and, None, ["lc"], ["li0"])
         ts(T.li[:, 12:24], T.lc[:], 6, None, ALU.logical_shift_right, None, ["lc"], ["li1"])
-        if t < R - 1:
-            a = 4 * (196 + 128 * (t + 1) + 64)
-            fill(tw[:, a:a + 256], 0.0, "z%d" % (t + 3))
-            spread_w(t + 1)
-        copy(T[ofl][:], T.li[:], ["li0", "li1"], [ofl])
-        copy(T.lf[0:32, 0:24], T.li[0:32, :], ["li0", "li1"], ["lf"])
         if t == 0:
-            for b in range(4):
-                quant("kf", 128 * b, 128 * b + 128, T.et2[:, 4 - b:516 - b], ["et2"], ["kf%d" % b])
-        op("v", lambda: V.transpose(T.lt[0:32, :], T.lf[0:32, :]), ["lf", "lfpad"], ["lt"])
-        dma("s", T.lv[t], T.lt[0:24, 0:16], ["lt"], ["lv%d" % t])
+            quant("kf", 384, 512, T.et2[:, 1:513], ["et2"], ["kf3"])
+        copy(T[ofl][:], T.li[:], ["li0", "li1"], [ofl])
+        if t < R - 1:
+            zeros_w6(t + 1)
+            spread_w(t + 1)
+
+        seen = set()
+
+        def unpack(r, b, start, stop):
+            c = cores[r]
+            if c == core:
+                mm("B%d" % b, "ke", 128 * b, rep, 0, 128, start, stop, ["ke%d" % b, rep + "q", rep + "s", rep + "pad"])
+            else:
+                extra = [] if r in seen else [("arr%d_%d" % (t, r), 2 * len(eng[c][core]))]
+                seen.add(r)
+                mm("B%d" % b, "ke", 128 * b, land, slot(c, core), 128, start, stop, ["ke%d" % b, land + "pad"], extra)
+
+        for b in (0, 1, 3, 2):
+            mm("A%d" % b, "ke", 128 * b, st, PAD, C, True, False, ["ke%d" % b] + both)
+        if t == 0:
+            fill(T.lf[0:32, 24:32], 0.0, "lfpad")
+        copy(T.lf[0:32, 0:24], T.li[0:32, :], ["li0", "li1"], ["lf"])
         if t < R - 1:
             quant_w6(t + 1)
+        op("v", lambda: V.transpose(T.lt[0:32, :], T.lf[0:32, :]), ["lf", "lfpad"], ["lt"])
         if t == 1:
             quant("kz", 0, 128, T.zt[:], ["zt"], ["kz"])
-
-        def unpack(r, start, stop):
-            c = cores[r]
-            for b in range(4):
-                if c == core:
-                    mm("B%d" % b, "ke", 128 * b, rep, 0, 128, start, stop, ["ke%d" % b, rep + "q", rep + "s", rep + "pad"])
-                else:
-                    extra = [("arr%d_%d" % (t, r), 2 * len(eng[c][core]))] if b == 0 else []
-                    mm("B%d" % b, "ke", 128 * b, land, slot(c, core), 128, start, stop, ["ke%d" % b, land + "pad"], extra)
-
         if early:
-            unpack(N - 1, True, True)
+            for b in range(4):
+                unpack(N - 1, b, True, True)
             for b in range(4):
                 act(T.dl[:, L * b:L * b + L], ps("B%d" % b, 0, L), ACT.Copy, [], ["B%d" % b, "dl%d" % b])
-            for r in range(N - 1):
-                unpack(r, r == 0, r == N - 2)
             for b in range(4):
+                for r in range(N - 1):
+                    unpack(r, b, r == 0, r == N - 2)
                 tt(T.vt[:, b:256:4], ps("B%d" % b, 0, L), T.dl[:, L * b:L * b + L], ALU.add, ["dl%d" % b], ["B%d" % b, "vt%d" % b])
         else:
-            for r in range(N):
-                unpack(r, r == 0, r == N - 1)
+            first = [rank, 1 - rank]
+            for k in range(2):
+                for b in range(4):
+                    unpack(first[k], b, k == 0, False)
             for b in range(4):
+                for r in range(2, N):
+                    unpack(r, b, False, r == N - 1)
                 if b % 2 == 0:
                     act(T.vt[:, b:256:4], ps("B%d" % b, 0, L), ACT.Copy, [], ["B%d" % b, "vt%d" % b])
                 else:
                     copy(T.vt[:, b:256:4], ps("B%d" % b, 0, L), [], ["B%d" % b, "vt%d" % b])
         quant(val, 0, 128, T.vt[:], ["vt0", "vt1", "vt2", "vt3", "vtpad"], [val])
+        dma("s", T.lv[t], T.lt[0:24, 0:16], ["lt", val], ["lv%d" % t])
         for b in range(4):
-            mm("B%d" % b, "ke", 128 * b, st, PAD + H, H, True, False, ["ke%d" % b, st + "1"])
+            mm("B%d" % b, "ke", 128 * b, st, PAD + C, TC - C, True, False, ["ke%d" % b] + both)
         for h in range(2):
-            pick(sel, H * h, H, val, L, ofl, 12 * h, [val, ofl], sel + str(h))
+            pick(sel, span[h][0], span[h][1], val, L, ofl, span[h][0] // 16, [val, ofl], sel + str(h))
         for h in range(2):
             for b in range(4):
-                mm("AB"[h] + str(b), "kf", 128 * b, sel, H * h, H, False, True, ["kf%d" % b, sel + str(h) + "q", sel + str(h) + "s"])
+                mm("AB"[h] + str(b), "kf", 128 * b, sel, span[h][0], span[h][1], False, True,
+                   ["kf%d" % b, sel + str(h) + "q", sel + str(h) + "s"])
 
         def drain(h, b, q):
-            a = 4 * (PAD + H * h) + b
+            a, n = 4 * (PAD + span[h][0]) + b, span[h][1]
             k = "AB"[h] + str(b)
             if q == "a":
-                act(hx[:, a:a + 4 * H - 3:4], ps(k, 0, H), ACT.Copy, [], [k, hxk[h][b]], scale=8.0)
+                act(hx[:, a:a + 4 * n - 3:4], ps(k, 0, n), ACT.Copy, [], [k, hxk[h][b]], scale=8.0)
             else:
-                ts(hx[:, a:a + 4 * H - 3:4], ps(k, 0, H), 8.0, None, ALU.mult, None, [], [k, hxk[h][b]])
+                ts(hx[:, a:a + 4 * n - 3:4], ps(k, 0, n), 8.0, None, ALU.mult, None, [], [k, hxk[h][b]])
 
-        for b in range(4):
-            drain(0, b, "va"[b % 2])
+        for h in range(2):
+            for b in range(4):
+                drain(h, b, DRAIN[4 * h + b])
         quant_state(t + 1, 0)
-        drain(1, 0, "a")
-        drain(1, 1, "a")
-        drain(1, 2, "v")
-        drain(1, 3, "a")
         if t == R - 1:
-            dma("s", T.oc[:, 0:4 * H], T[nxt + "q"][:, PAD:PAD + H].bitcast(dt.uint8), [nxt + "0"], ["oc0"])
-            mm("A0", "kz", 0, nxt, PAD, H, True, True, ["kz", nxt + "0"])
-            act(T.ysb[:, 0:H], ps("A0", 0, H), ACT.Copy, [], ["A0", "y0"])
-            dma("a", T.y[:, 0:H], T.ysb[:, 0:H], ["y0"], ["oy0"])
+            dma("s", T.oc[:, 0:4 * C], T[nxt + "q"][:, PAD:PAD + C].bitcast(dt.uint8), [nxt + "0"], ["oc0"])
+            mm("A0", "kz", 0, nxt, PAD, C, True, True, ["kz", nxt + "0"])
+            act(T.ysb[:, 0:C], ps("A0", 0, C), ACT.Copy, [], ["A0", "y0"])
+            dma("a", T.y[:, 0:C], T.ysb[:, 0:C], ["y0"], ["oy0"])
         quant_state(t + 1, 1)
 
     fin = "st%d" % R
-    mm("A1", "kz", 0, fin, PAD + H, H, True, True, ["kz", fin + "1"])
-    dma("s", T.oc[:, 4 * H:8 * H], T[fin + "q"][:, PAD + H:PAD + TC].bitcast(dt.uint8), [fin + "1"], ["oc1"])
-    copy(T.ysb[:, H:TC], ps("A1", 0, H), [], ["A1", "y1"])
+    mm("A1", "kz", 0, fin, PAD + C, TC - C, True, True, ["kz", fin + "1"])
+    dma("s", T.oc[:, 4 * C:4 * TC], T[fin + "q"][:, PAD + C:PAD + TC].bitcast(dt.uint8), [fin + "1"], ["oc1"])
+    copy(T.ysb[:, C:TC], ps("A1", 0, TC - C), [], ["A1", "y1"])
     for k in range(2):
         dma("a", T.osc[4 * k:4 * k + 4, :], T[fin + "s"][32 * k:32 * k + 4, PAD:PAD + TC], [fin + "0", fin + "1"], ["os%d" % k])
-    dma("s", T.y[:, H:TC], T.ysb[:, H:TC], ["y1"], ["oy1"])
+    dma("s", T.y[:, C:TC], T.ysb[:, C:TC], ["y1"], ["oy1"])
     for k in range(2, 4):
         dma("a", T.osc[4 * k:4 * k + 4, :], T[fin + "s"][32 * k:32 * k + 4, PAD:PAD + TC], [fin + "0", fin + "1"], ["os%d" % k])
     op("g", None, extra=[("sent", sent)], dma=True)

@@ -12,15 +12,15 @@ SCRATCH = {
     "bt": ("sbuf", [128, 4 * H], BF), "cg": ("sbuf", [128, 512], BF), "ci": ("sbuf", [128, 512], BF),
     "cl": ("sbuf", [128, 512], BF), "et": ("sbuf", [128, 520], BF), "et2": ("sbuf", [128, 520], BF),
     "vt": ("sbuf", [128, 512], BF), "zt": ("sbuf", [128, 512], BF), "jm": ("sbuf", [128, H], BF),
-    "etr": ("sbuf", [128, 520], BF), "low": ("sbuf", [128, H], BF), "junk": ("sbuf", [128, H + PAD], BF),
-    "d0": ("sbuf", [128, H], BF),
+    "etr": ("sbuf", [128, 520], BF), "low": ("sbuf", [128, H], BF), "junk": ("sbuf", [128, 16], BF),
+    "jnk2": ("sbuf", [128, H + PAD], BF), "d0": ("sbuf", [128, H], BF),
     "aip": ("sbuf", [128, 8], I32), "aik": ("sbuf", [128, 8], I32), "im": ("sbuf", [128, L], I32),
     "iv": ("sbuf", [128, L], I32), "iv2": ("sbuf", [128, L], I32),
     "ipen": ("sbuf", [128, 4], I32), "apen": ("sbuf", [128, 4], I32), "lc": ("sbuf", [128, 12], I32),
     "li": ("sbuf", [128, 24], I32),
     "f1": ("sbuf", [128, 8], F32), "f2": ("sbuf", [128, 8], F32), "col": ("sbuf", [128, 32], F32),
     "pen": ("sbuf", [128, 4], F32), "mc": ("sbuf", [128, 4], F32), "pc": ("sbuf", [128, 4], F32),
-    "run": ("sbuf", [128, H + PAD], F32), "cnt": ("sbuf", [128, 8], F32),
+    "run": ("sbuf", [128, H + PAD], F32), "cnt": ("sbuf", [128, 12], F32),
     "ls": ("sbuf", [128, H], F32), "lf": ("sbuf", [128, 32], F32),
     "lt": ("sbuf", [128, 32], F32), "ysb": ("sbuf", [128, TC], F32), "dl": ("sbuf", [128, 4 * L], F32),
 }
@@ -36,8 +36,7 @@ for _n, _w in (("w", 576), ("b", H), ("i", 128), ("cg", 128), ("ci", 128), ("cl"
 for _t in range(R + 1):
     _pair("st%d" % _t, TC + PAD)
 for _t in range(R):
-    _pair("rep%d" % _t, 192)
-    _pair("land%d" % _t, 320)
+    _pair("land%d" % _t, 384)
     _pair("val%d" % _t, 128)
     _pair("sel%d" % _t, TC)
     SCRATCH["ofr%d" % _t] = ("sbuf", [128, 4], U16)
@@ -49,28 +48,33 @@ SEMAPHORES = (["c%d" % k for k in range(NC)] + ["d%d" % k for k in range(ND)]
 
 BIT = 2.0 ** 26
 FLOOR = -2.0 ** 70
-MAGIC = 1.5 * 2.0 ** 27
-CUT = (192, 192, 192, 192)
-DRAIN = "vavavava"
+MAGIC = 1.5 * 2.0 ** 28
+CUT = (256, 192, 192, 160)
 
 
-def engine_sets(src, cores, topo):
-    peers = [c for c in cores if c != src]
-    far = [c for c in peers if topo.chip(c) != topo.chip(src)]
-    near = [c for c in peers if topo.chip(c) == topo.chip(src)]
-    out = {}
-    used = []
-    if far:
-        used = topo.engines(src, far[0])
-        k = len(used) // len(far)
-        for n, c in enumerate(far):
-            out[c] = used[n * k:(n + 1) * k]
-    if near:
-        rest = [e for e in topo.engines(src, near[0]) if e not in used]
-        k = len(rest) // len(near)
-        for n, c in enumerate(near):
-            out[c] = rest[n * k:(n + 1) * k]
-    return out
+def exchange_plan(cores, topo):
+    n = len(cores)
+    plan = []
+    for r, c in enumerate(cores):
+        home = [k for k in range(n) if topo.chip(cores[k]) == topo.chip(c)]
+        far = [k for k in range(n) if k not in home]
+        i = home.index(r)
+        early, late = far[i], far[1 - i]
+        near = home[1 - i]
+        held = None if late == n - 1 else n - 1
+        pre = [1 - late] if late < 2 else sorted(range(late), key=lambda k: (k != r, k != near))
+        post = [k for k in range(late, n) if k not in pre and k != held]
+        if held is None or held == r:
+            slots = [late] + [k for k in post[1:] if k != r] + [k for k in pre[::-1] if k != r]
+        else:
+            slots = [late] + [k for k in pre if k != r] + [held]
+        out = topo.engines(c, cores[early])
+        rest = [e for e in topo.engines(c, cores[near]) if e not in out]
+        k = len(out) // 2
+        tail = [("s", {early: out[:k], late: out[k:], near: rest}), ("q", {late: out})]
+        calls = [[("q", {early: out}), ("q", {near: rest})] + tail] + [[("q", {early: out, near: rest})] + tail] * (R - 1)
+        plan.append({"pre": pre, "post": post, "held": held, "slots": slots + [r], "calls": calls})
+    return plan
 
 
 def emit_program(ops, queues, T):
@@ -131,7 +135,6 @@ def rank_program(g, core, T, topo):
     if rank is None:
         return
     cores = list(T.cores)
-    N = len(cores)
     V, A, P, S = g.vector, g.scalar, g.tensor, g.sync
     queues = {"g": g, "v": V, "a": A, "p": P, "s": S}
     ops = []
@@ -187,15 +190,12 @@ def rank_program(g, core, T, topo):
                                       T[src + "q"][:, 0:width].bitcast(dt.uint32).indirect(o)), r, [w + "q"])
         op("a", lambda: A.activation(T[dst + "s"][:, a:a + n], T[src + "s"][:, 0:width].indirect(o), ACT.Copy), r, [w + "s"])
 
-    def slot(sender, receiver):
-        order = [o for o in cores if o != receiver]
-        if topo.chip(cores[-1]) == topo.chip(receiver) and cores[-1] in order:
-            order = order[-1:] + order[:-1]
-        return L * (len(order) - 1 - order.index(sender))
-
     tw, hx, col = T.tw, T.hx, T.col
     hxk = [["hx%d%d" % (h, b) for b in range(4)] for h in range(2)]
-    PW, S1, R32, HS, PW2R, PW2 = [col[:, 4 * k:4 * k + 1] for k in range(6)]
+    PW, S1, R32, PW2R, PW2 = [col[:, 4 * k:4 * k + 1] for k in (0, 1, 2, 4, 5)]
+
+    def zeros(out, w):
+        act(out, tw[:, 16:272], ACT.Copy, ["z0"], w)
 
     def spread_w(t):
         for e in range(4):
@@ -209,200 +209,223 @@ def rank_program(g, core, T, topo):
 
     def zeros_w6(t):
         a = 4 * (196 + 128 * t + 64)
-        act(tw[:, a:a + 256], tw[:, 16:272], ACT.Copy, ["z0"], ["z%d" % (t + 2)])
+        zeros(tw[:, a:a + 256], ["z%d" % (t + 2)])
 
     def quant_state(t, h):
         a, b = (0, PAD + CUT[t]) if h == 0 else (PAD + CUT[t], PAD + TC)
         quant("st%d" % t, a, b, hx[:, 4 * a:4 * b], hxk[h] + (["hxpad"] if h == 0 else []), ["st%d%d" % (t, h)])
 
-    dma("a", tw[:, 272:528], T.w[:, 0:256], [], ["wp"])
-    dma("s", hx[:, 8:8 + 4 * CUT[0]], T.x[:, 0:4 * CUT[0]], [], hxk[0])
-    dma("s", hx[:, 8 + 4 * CUT[0]:8 + 4 * TC], T.x[:, 4 * CUT[0]:4 * TC], [], hxk[1])
-    iota(T.aip[:, 0:6], [[1, 6]], 0, 1, ["aip"], True)
-    iota(T.pc[:, 0:2], [[0, 2]], -15, 2, ["pc"])
-    iota(T.im[:], [[1, L]], 0, 0, ["im"], True)
-    iota(T.jm[:], [[0, 12], [-2, 16]], 0, 2, ["jm"])
-    iota(T.cg[:], [[0, 512]], 0, 0, ["cg0", "cg1", "cg2", "cg3"])
-    iota(T.ipen[:], [[-16, 4]], 64, 1, ["ipen"], True)
-    iota(T.etr[:], [[-1, 520]], 4, 4, ["etr"])
-    iota(T.d0[:], [[0, 12], [1, 16]], 0, 0, ["d0r"])
-    aik = ["aik"]
-    fill(tw[:, 0:272], 0.0, "z0", "it0", "it1", "it2a", "it2b")
-    fill(tw[:, 528:784], 0.0, "z1")
-    ts(T.aik[:, 0:6], T.aip[:, 0:6], 63, None, ALU.bitwise_and, None, ["aip"], aik)
-    zeros_w6(0)
-    act(T.vt[:, 256:512], tw[:, 16:272], ACT.Copy, ["z0"], ["vtpad"])
-    ts(R32, T.pc[:, 0:1], 2 * MAGIC, 2 * MAGIC, ALU.add, ALU.subtract, ["pc"], ["r32"])
-    ts(T.f1[:, 0:5], T.aik[:, 0:5], 5.0, 1.0, ALU.is_lt, ALU.add, aik, ["f1"])
-    ts(S1, T.aik[:, 0:1], 6.0, 2.0 ** 42, ALU.is_lt, ALU.mult, aik, ["s1"])
-    op("v", lambda: V.tensor_reduce(PW, T.f1[:, 0:5], AxisListType.X, ALU.mult), ["f1"], ["pw"])
-    ts(T.f2[:, 0:5], T.aik[:, 0:5], 5.0, 1.0, ALU.is_ge, ALU.add, aik, ["f2"])
-    ts(T.iv[:], T.im[:], PW, None, ALU.mult, None, ["im", "pw"], ["iv"])
-    fill(T.bt[:, 1:4 * H:2], BIT, "bt1")
-    ts(T.iv2[:], T.iv[:], 32, None, ALU.bitwise_and, None, ["iv"], ["iv2"])
-    ts(T.bt[:, 2:4 * H:4], T.jm[:], R32, BIT, ALU.is_equal, ALU.mult, ["jm", "r32"], ["bt2"])
-    fill(hx[:, 0:8], 0.0, "hxpad")
-    op("v", lambda: V.tensor_reduce(PW2R, T.f2[:, 0:5], AxisListType.X, ALU.mult), ["f2"], ["pw2r"])
-    spread_w(0)
-    for e in (0, 1, 3):
-        act(T.ci[:, e:512:4], T.bt[:, 2:512:4], ACT.Copy, ["bt2"], ["ci%d" % e], scale=1 / BIT)
-    for h in range(2):
-        act(T.ci[64 * h:64 * h + 64, 2:512:4], T.bt[64 * h:64 * h + 64, 2:512:4], ACT.Copy, ["bt2"], ["ci2%d" % h], scale=h * H / BIT)
-    quant("kw", 0, 192, tw[:, 16:784], ["z0", "wp", "z1"], ["kw0"])
-    fill(T.low[:], FLOOR, "low")
-    fill(T.run[:, 0:PAD], FLOOR, "runpad")
-    quant_w6(0)
+    def quant_e(name, tile, b):
+        quant(name, 128 * b, 128 * b + 128, T[tile][:, 4 - b:516 - b], [tile], [name + str(b)])
 
     def member(h):
         p0, p1, a = 64 * h, 64 * h + 64, 256 * h
         ts(T.cg[p0:p1, a:a + 256:4], T.iv2[p0:p1, :], 16.0, col[p0:p1, 4:5], ALU.subtract, ALU.mult, ["iv2", "s1"], ["cg%d" % (2 * h)])
         ts(T.cg[p0:p1, a + 1:a + 256:4], T.iv2[p0:p1, :], col[p0:p1, 4:5], -0.5, ALU.mult, ALU.mult, ["iv2", "s1"], ["cg%d" % (2 * h + 1)])
 
+    dma("a", tw[:, 272:368], T.w[:, 0:96], [], ["wp"])
+    dma("s", hx[:, 8:8 + 4 * CUT[0]], T.x[:, 0:4 * CUT[0]], [], hxk[0])
+    dma("s", hx[:, 8 + 4 * CUT[0]:8 + 4 * TC], T.x[:, 4 * CUT[0]:4 * TC], [], hxk[1])
+    iota(T.aip[:, 0:6], [[1, 6]], 0, 1, ["aip"], True)
+    iota(T.pc[:, 0:2], [[0, 2]], -15, 2, ["pc"])
+    iota(T.im[:], [[1, L]], 0, 0, ["im"], True)
+    iota(T.jm[:], [[0, 12], [-2, 16]], 0, 2, ["jm"])
+    iota(T.etr[:], [[-1, 520]], 4, 4, ["etr"])
+    iota(T.ipen[:], [[-16, 4]], 64, 1, ["ipen"], True)
+    iota(T.d0[:], [[0, 12], [1, 16]], 0, 0, ["d0r"])
+    aik = ["aik"]
+    fill(tw[:, 0:272], 0.0, "z0", "it0", "it1", "it2a", "it2b")
+    fill(tw[:, 368:784], 0.0, "z1")
+    ts(T.aik[:, 0:6], T.aip[:, 0:6], 63, None, ALU.bitwise_and, None, ["aip"], aik)
+    zeros_w6(0)
+    zeros(T.cg[:, 0:256], ["cg0", "cg1"])
+    zeros(T.cg[:, 256:512], ["cg2", "cg3"])
+    fill(hx[:, 0:8], 0.0, "hxpad")
+    ts(R32, T.pc[:, 0:1], MAGIC, MAGIC, ALU.add, ALU.subtract, ["pc"], ["r32"])
+    ts(T.f1[:, 0:5], T.aik[:, 0:5], 5.0, 1.0, ALU.is_lt, ALU.add, aik, ["f1"])
+    ts(S1, T.aik[:, 0:1], 6.0, 2.0 ** 42, ALU.is_lt, ALU.mult, aik, ["s1"])
+    ts(T.f2[:, 0:5], T.aik[:, 0:5], 5.0, 1.0, ALU.is_ge, ALU.add, aik, ["f2"])
+    op("v", lambda: V.tensor_reduce(PW, T.f1[:, 0:5], AxisListType.X, ALU.mult), ["f1"], ["pw"])
+    fill(T.bt[:, 1:4 * H:2], BIT, "bt1")
+    ts(T.iv[:], T.im[:], PW, None, ALU.mult, None, ["im", "pw"], ["iv"])
+    ts(T.bt[:, 2:4 * H:4], T.jm[:], R32, BIT, ALU.is_equal, ALU.mult, ["jm", "r32"], ["bt2"])
+    op("v", lambda: V.tensor_reduce(PW2R, T.f2[:, 0:5], AxisListType.X, ALU.mult), ["f2"], ["pw2r"])
+    ts(T.iv2[:], T.iv[:], 32, None, ALU.bitwise_and, None, ["iv"], ["iv2"])
+    spread_w(0)
+    for e in (0, 1, 3):
+        act(T.ci[:, e:512:4], T.bt[:, 2:512:4], ACT.Copy, ["bt2"], ["ci%d" % e], scale=1 / BIT)
+    for h in range(2):
+        act(T.ci[64 * h:64 * h + 64, 2:512:4], T.bt[64 * h:64 * h + 64, 2:512:4], ACT.Copy, ["bt2"], ["ci2%d" % h], scale=h * H / BIT)
+    quant("kw", 0, 192, tw[:, 16:784], ["z0", "wp", "z1"], ["kw0"])
     member(0)
     quant_state(0, 0)
-    member(1)
     quant_state(0, 1)
     dma("s", T.zt[:], T.z[:], ["st01"], ["zt"])
+    member(1)
+    quant_w6(0)
     act(T.et2[:], T.etr[:], ACT.Abs, ["etr"], ["et2"])
     act(T.et[:], T.et2[:], ACT.Relu, ["et2"], ["et"], scale=-0.125, bias=0.125)
+    for k in range(2):
+        zeros(T.cl[:, 256 * k:256 * k + 256], ["clz%d" % k])
 
-    eng = {c: engine_sets(c, cores, topo) for c in cores}
-    others = [o for o in cores if o != core]
-    early = topo.chip(cores[-1]) == topo.chip(core)
+    plan = exchange_plan(cores, topo)
+    me = plan[rank]
+    aside = me["held"] not in (None, rank)
+    own = L * me["slots"].index(rank)
     sent = 0
     bts = ["bt0", "bt1", "bt2"]
+    top = PAD + H - 1
     for t in range(R):
-        st, nxt, rep, land, val, sel = ["%s%d" % (s, k) for s, k in
-                                        (("st", t), ("st", t + 1), ("rep", t), ("land", t), ("val", t), ("sel", t))]
+        st, nxt, land, val, sel = ["%s%d" % (s, k) for s, k in (("st", t), ("st", t + 1), ("land", t), ("val", t), ("sel", t))]
         ofr, ofl = "ofr%d" % t, "ofl%d" % t
         C = CUT[t + 1]
         span = ((0, C), (C, TC - C))
         both = [st + "0", st + "1"]
         kwp = ["kw0", "kw1"] if t else ["kw0"]
         kws = ["kw%d" % t, "kw%d" % (t + 1)]
+
+        def pad_land():
+            quant(land, 256, 384, tw[:, 528:1040], ["z1", "kw1"], [land + "pad"])
+
+        def leaf_product():
+            mm("A2", "kcl", 0, "kb", 0, H, True, True, ["kcl", "kb"])
+
+        def leaf_scan():
+            op("v", lambda: V.tensor_tensor_scan(T.ls[:], T.d0[:], ps("A2", 0, H), 0.0, ALU.mult, ALU.max), ["d0"], ["A2", "ls"])
+
+        if t:
+            quant_w6(t)
         mm("A0", "kw", 64 + 8 * t, st, PAD, H, True, False, kwp + [st + "0"])
         mm("A0", "kw", 8 * t, st, PAD + H, H, False, True, kwp + both)
         mm("A1", "kw", 192 + 128 * t, st, PAD, H, True, False, kws + both)
         mm("A1", "kw", 128 + 128 * t, st, PAD + H, H, False, False, kws + both)
         if t == 0:
             quant("kcg", 0, 128, T.cg[:], ["cg0", "cg1", "cg2", "cg3"], ["kcg"])
-            ts(T.apen[:], T.ipen[:], 48, None, ALU.bitwise_and, None, ["ipen"], ["apen"])
         ts(T.bt[:, 0:4 * H:4], ps("A0", 0, H), 0.0, BIT, ALU.is_lt, ALU.mult, [], ["A0", "bt0"])
+        if t == 0:
+            ts(T.apen[:], T.ipen[:], 48, None, ALU.bitwise_and, None, ["ipen"], ["apen"])
         quant("kb", 0, H, T.bt[:], bts, ["kb"])
         mm("A1", "kcg", 0, "kb", 0, H, False, True, ["kcg", "kb"])
         if t == 0:
             ts(T.pen[:], T.apen[:], 0.0, -2.0 ** 80, ALU.not_equal, ALU.mult, ["apen"], ["pen"])
-            quant("kci", 0, 128, T.ci[:], ["ci0", "ci1", "ci20", "ci21", "ci3"], ["kci"])
+            fill(T.low[:], FLOOR, "low")
+            fill(T.run[:, 0:PAD], FLOOR, "runpad")
+            fill(T.mc[:], 16.0, "mc")
+        else:
+            pad_land()
+            leaf_product()
         op("v", lambda: V.tensor_tensor_scan(T.run[:, PAD:], ps("A1", 0, H), T.low[:], FLOOR, ALU.max, ALU.max), ["low"], ["A1", "run"])
         if t == 0:
-            fill(T.mc[:], MAGIC, "mc")
-        top = PAD + H - 1
-        act(T.junk[:], T.run[:], ACT.Sign, ["run", "runpad"], ["junk", "cnt"], bias=T.run[:, top:top + 1], scale=-1.0,
+            quant("kci", 0, 128, T.ci[:], ["ci0", "ci1", "ci20", "ci21", "ci3"], ["kci"])
+        act(T.junk[:, 0:12], T.run[:, 15:top:16], ACT.Sign, ["run"], ["junk0", "hi"], bias=T.run[:, top:top + 1], scale=-1.0,
+            accum_out=T.cnt[:, 4:5])
+        act(T.jnk2[:], T.run[:], ACT.Sign, ["run", "runpad"], ["junk", "cnt"], bias=T.run[:, top:top + 1], scale=-1.0,
             accum_out=T.cnt[:, 0:1])
         ts(tw[0:64, 2:16:4], T.pen[0:64, :], T.run[0:64, top:top + 1], T.run[64:128, top:top + 1], ALU.add, ALU.is_ge,
            ["pen", "run"], ["it2a"])
         ts(tw[64:128, 2:16:4], T.pen[64:128, :], T.run[64:128, top:top + 1], T.run[0:64, top:top + 1], ALU.add, ALU.is_gt,
            ["pen", "run"], ["it2b"])
-        ts(T.cnt[:, 4:5], T.cnt[:, 0:1], MAGIC, MAGIC, ALU.add, ALU.subtract, ["cnt"], ["hi"])
-        ts(tw[:, 0:16:4], T.mc[:], T.cnt[:, 0:1], MAGIC, ALU.add, ALU.subtract, ["mc", "cnt"], ["it0"])
-        ts(tw[:, 1:16:4], tw[:, 2:16:4], T.cnt[:, 0:1], T.cnt[:, 4:5], ALU.mult, ALU.subtract, ["cnt", "hi", "it2a", "it2b"], ["it1"])
-        quant("ki", 0, 128, tw[:, 0:512], ["it0", "it1", "it2a", "it2b", "z0", "wp"], ["ki"])
+        ts(T.cnt[:, 8:9], T.cnt[:, 4:5], 16.0, None, ALU.mult, None, ["hi"], ["hi16"])
+        ts(tw[:, 0:16:4], T.mc[:], T.cnt[:, 4:5], None, ALU.mult, None, ["mc", "hi"], ["it0"])
+        ts(tw[:, 1:16:4], tw[:, 2:16:4], T.cnt[:, 0:1], T.cnt[:, 8:9], ALU.mult, ALU.subtract, ["cnt", "hi16", "it2a", "it2b"], ["it1"])
+        quant("ki", 0, 128, tw[:, 0:512], ["it0", "it1", "it2a", "it2b", "z0", "z1", "wp"], ["ki"])
         mm("A3", "kci", 0, "ki", 0, 128, True, True, ["kci", "ki"])
         if t == 0:
-            quant("ke", 0, 128, T.et[:, 4:516], ["et"], ["ke0"])
+            quant_e("ke", "et", 0)
+            quant_e("ke", "et", 1)
+        else:
+            leaf_scan()
         copy(T[ofr][:], ps("A3", 0, 4), [], ["A3", ofr])
-        pick(rep, 0, L, st, TC + PAD, ofr, 0, both + [ofr], rep)
-        for kind in "qs":
+        pick(land, own, L, st, TC + PAD, ofr, 0, both + [ofr], land)
+        for kind, peers in me["calls"][t]:
             trs = []
-            for c in others:
-                pos = slot(core, c)
-                rid, pid, _ = topo.addr(c)
-                mask = sum(1 << e for e in eng[core][c])
-                src, dst = T[rep + kind][:, 0:L], T[land + kind][:, pos:pos + L]
+            for r in peers:
+                pos = L * plan[r]["slots"].index(rank)
+                rid, pid, _ = topo.addr(cores[r])
+                src, dst = T[land + kind][:, own:own + L], T[land + kind][:, pos:pos + L]
                 if kind == "q":
                     src, dst = src.bitcast(dt.uint8), dst.bitcast(dt.uint8)
-                trs.append(RemoteDMATransfer(dst_ids=[DstId(rid=rid, pnc=pid)], dma_engine_mask=mask,
+                trs.append(RemoteDMATransfer(dst_ids=[DstId(rid=rid, pnc=pid)], dma_engine_mask=sum(1 << e for e in peers[r]),
                                              remote_sem=T.sem["arr%d_%d" % (t, rank)], src=src, dst=dst))
-                sent += len(eng[core][c])
-            op("g", lambda trs=trs: g.remote_dma_fused(trs, local_sem=T.sem.sent), [rep + kind], [], dma=True)
+                sent += len(peers[r])
+            op("g", lambda trs=trs: g.remote_dma_fused(trs, local_sem=T.sem.sent), [land + kind], [], dma=True)
         if t == 0:
-            fill(T.cl[:], 0.0, "cl0", "cl2")
             for h in range(2):
                 ts(col[64 * h:64 * h + 64, 20:21], col[64 * h:64 * h + 64, 16:17], col[64 * h:64 * h + 64, 4:5], 2.0 ** (6 * h - 68),
                    ALU.mult, ALU.mult, ["pw2r", "s1"], ["pw2%d" % h])
-            act(T.et2[:], T.et[:], ACT.Copy, ["et"], ["et2"], scale=-0.5)
-            act(T.cl[32:48, 2:512:4], T.ci[32:48, 0:512:4], ACT.Identity, ["ci0"], ["cl2"], scale=2.0 ** -14, bias=-2.0 ** -14)
-            act(T.cl[:, 0:512:4], T.ci[:, 0:512:4], ACT.Identity, ["ci0", "pw20", "pw21"], ["cl0"], scale=0.0, bias=PW2)
+            act(T.cl[32:48, 2:512:4], T.ci[32:48, 0:512:4], ACT.Identity, ["ci0", "clz0", "clz1"], ["cl2"], scale=2.0 ** -14, bias=-2.0 ** -14)
+            act(T.cl[:, 0:512:4], T.ci[:, 0:512:4], ACT.Identity, ["ci0", "pw20", "pw21", "clz0", "clz1"], ["cl0"], scale=0.0, bias=PW2)
             act(T.d0[:], T.d0[:], ACT.Sign, ["d0r"], ["d0"])
-            for b in range(1, 4):
-                quant("ke", 128 * b, 128 * b + 128, T.et[:, 4 - b:516 - b], ["et"], ["ke%d" % b])
-        quant(land, 192, 320, T.bt[:, 0:512], bts, [land + "pad"])
-        quant(rep, 64, 192, T.bt[:, 0:512], bts, [rep + "pad"])
-        if t == 0:
+            act(T.et2[:], T.et[:], ACT.Copy, ["et"], ["et2"], scale=-0.5)
+            zeros(T.vt[:, 256:512], ["vtpad"])
+            pad_land()
+            quant_e("ke", "et", 2)
+            quant_e("ke", "et", 3)
             quant("kcl", 0, 128, T.cl[:], ["cl0", "cl2"], ["kcl"])
-        mm("A2", "kcl", 0, "kb", 0, H, True, True, ["kcl", "kb"])
-        op("v", lambda: V.tensor_tensor_scan(T.ls[:], T.d0[:], ps("A2", 0, H), 0.0, ALU.mult, ALU.max), ["d0"], ["A2", "ls"])
-        if t == 0:
-            for b in range(2):
-                quant("kf", 128 * b, 128 * b + 128, T.et2[:, 4 - b:516 - b], ["et2"], ["kf%d" % b])
+            leaf_product()
+            leaf_scan()
+            quant_e("kf", "et2", 0)
         copy(T.lc[:], T.ls[:, 15:H:16], ["ls"], ["lc"])
         if t == 0:
-            quant("kf", 256, 384, T.et2[:, 2:514], ["et2"], ["kf2"])
+            quant_e("kf", "et2", 1)
+        if t == 1:
+            quant("kz", 0, 128, T.zt[:], ["zt"], ["kz"])
         ts(T.li[:, 0:12], T.lc[:], 63, None, ALU.bitwise_and, None, ["lc"], ["li0"])
         ts(T.li[:, 12:24], T.lc[:], 6, None, ALU.logical_shift_right, None, ["lc"], ["li1"])
         if t == 0:
-            quant("kf", 384, 512, T.et2[:, 1:513], ["et2"], ["kf3"])
+            quant_e("kf", "et2", 2)
+            fill(T.lf[0:32, 24:32], 0.0, "lfpad")
         copy(T[ofl][:], T.li[:], ["li0", "li1"], [ofl])
+        copy(T.lf[0:32, 0:24], T.li[0:32, :], ["li0", "li1"], ["lf"])
+        if t == 0:
+            quant_e("kf", "et2", 3)
+        op("v", lambda: V.transpose(T.lt[0:32, :], T.lf[0:32, :]), ["lf", "lfpad"], ["lt"])
         if t < R - 1:
             zeros_w6(t + 1)
             spread_w(t + 1)
 
-        seen = set()
+        seen = {rank}
 
-        def unpack(r, b, start, stop):
-            c = cores[r]
-            if c == core:
-                mm("B%d" % b, "ke", 128 * b, rep, 0, 128, start, stop, ["ke%d" % b, rep + "q", rep + "s", rep + "pad"])
-            else:
-                extra = [] if r in seen else [("arr%d_%d" % (t, r), 2 * len(eng[c][core]))]
-                seen.add(r)
-                mm("B%d" % b, "ke", 128 * b, land, slot(c, core), 128, start, stop, ["ke%d" % b, land + "pad"], extra)
+        def unpack(r, b, start, stop, bk="B"):
+            k = me["slots"].index(r)
+            extra = [("arr%d_%d" % (t, o), sum(len(p.get(rank, ())) for _, p in plan[o]["calls"][t]))
+                     for o in me["slots"][k:k + 2] if o not in seen]
+            seen.update(me["slots"][k:k + 2])
+            mm(bk + str(b), "ke", 128 * b, land, L * k, 128, start, stop, ["ke%d" % b, land + "q", land + "s", land + "pad"], extra)
 
-        for b in (0, 1, 3, 2):
-            mm("A%d" % b, "ke", 128 * b, st, PAD, C, True, False, ["ke%d" % b] + both)
-        if t == 0:
-            fill(T.lf[0:32, 24:32], 0.0, "lfpad")
-        copy(T.lf[0:32, 0:24], T.li[0:32, :], ["li0", "li1"], ["lf"])
-        if t < R - 1:
-            quant_w6(t + 1)
-        op("v", lambda: V.transpose(T.lt[0:32, :], T.lf[0:32, :]), ["lf", "lfpad"], ["lt"])
-        if t == 1:
-            quant("kz", 0, 128, T.zt[:], ["zt"], ["kz"])
-        if early:
+        def hold(bk):
             for b in range(4):
-                unpack(N - 1, b, True, True)
+                unpack(me["held"], b, True, True, bk)
             for b in range(4):
-                act(T.dl[:, L * b:L * b + L], ps("B%d" % b, 0, L), ACT.Copy, [], ["B%d" % b, "dl%d" % b])
+                act(T.dl[:, L * b:L * b + L], ps(bk + str(b), 0, L), ACT.Copy, [], [bk + str(b), "dl%d" % b])
+
+        def load(h, bs):
+            for b in bs:
+                mm("AB"[h] + str(b), "ke", 128 * b, st, PAD + span[h][0], span[h][1], True, False, ["ke%d" % b] + both)
+
+        if not aside:
+            load(0, (0, 1, 3, 2))
+        if me["held"] == rank:
+            hold("B")
+        for k, r in enumerate(me["pre"]):
             for b in range(4):
-                for r in range(N - 1):
-                    unpack(r, b, r == 0, r == N - 2)
+                unpack(r, b, k == 0, False)
+            if aside and k == 0:
+                hold("A")
+        for b in range(4):
+            for r in me["post"]:
+                unpack(r, b, False, r == me["post"][-1])
+            if me["held"] is not None:
                 tt(T.vt[:, b:256:4], ps("B%d" % b, 0, L), T.dl[:, L * b:L * b + L], ALU.add, ["dl%d" % b], ["B%d" % b, "vt%d" % b])
-        else:
-            first = [rank, 1 - rank]
-            for k in range(2):
-                for b in range(4):
-                    unpack(first[k], b, k == 0, False)
-            for b in range(4):
-                for r in range(2, N):
-                    unpack(r, b, False, r == N - 1)
-                if b % 2 == 0:
-                    act(T.vt[:, b:256:4], ps("B%d" % b, 0, L), ACT.Copy, [], ["B%d" % b, "vt%d" % b])
-                else:
-                    copy(T.vt[:, b:256:4], ps("B%d" % b, 0, L), [], ["B%d" % b, "vt%d" % b])
+            elif b % 2 == 0:
+                act(T.vt[:, b:256:4], ps("B%d" % b, 0, L), ACT.Copy, [], ["B%d" % b, "vt%d" % b])
+            else:
+                copy(T.vt[:, b:256:4], ps("B%d" % b, 0, L), [], ["B%d" % b, "vt%d" % b])
+        if aside:
+            load(0, range(4))
         quant(val, 0, 128, T.vt[:], ["vt0", "vt1", "vt2", "vt3", "vtpad"], [val])
         dma("s", T.lv[t], T.lt[0:24, 0:16], ["lt", val], ["lv%d" % t])
-        for b in range(4):
-            mm("B%d" % b, "ke", 128 * b, st, PAD + C, TC - C, True, False, ["ke%d" % b] + both)
+        load(1, range(4))
         for h in range(2):
             pick(sel, span[h][0], span[h][1], val, L, ofl, span[h][0] // 16, [val, ofl], sel + str(h))
         for h in range(2):
@@ -410,23 +433,30 @@ def rank_program(g, core, T, topo):
                 mm("AB"[h] + str(b), "kf", 128 * b, sel, span[h][0], span[h][1], False, True,
                    ["kf%d" % b, sel + str(h) + "q", sel + str(h) + "s"])
 
-        def drain(h, b, q):
+        def drain(h, b):
             a, n = 4 * (PAD + span[h][0]) + b, span[h][1]
             k = "AB"[h] + str(b)
-            if q == "a":
+            if b % 2:
                 act(hx[:, a:a + 4 * n - 3:4], ps(k, 0, n), ACT.Copy, [], [k, hxk[h][b]], scale=8.0)
             else:
                 ts(hx[:, a:a + 4 * n - 3:4], ps(k, 0, n), 8.0, None, ALU.mult, None, [], [k, hxk[h][b]])
 
-        for h in range(2):
+        for b in range(4):
+            drain(0, b)
+        if t < R - 1:
             for b in range(4):
-                drain(h, b, DRAIN[4 * h + b])
-        quant_state(t + 1, 0)
-        if t == R - 1:
+                drain(1, b)
+            quant_state(t + 1, 0)
+        else:
+            drain(1, 0)
+            drain(1, 1)
+            quant_state(t + 1, 0)
             dma("s", T.oc[:, 0:4 * C], T[nxt + "q"][:, PAD:PAD + C].bitcast(dt.uint8), [nxt + "0"], ["oc0"])
             mm("A0", "kz", 0, nxt, PAD, C, True, True, ["kz", nxt + "0"])
+            drain(1, 2)
+            drain(1, 3)
             act(T.ysb[:, 0:C], ps("A0", 0, C), ACT.Copy, [], ["A0", "y0"])
-            dma("a", T.y[:, 0:C], T.ysb[:, 0:C], ["y0"], ["oy0"])
+            dma("s", T.y[:, 0:C], T.ysb[:, 0:C], ["y0"], ["oy0"])
         quant_state(t + 1, 1)
 
     fin = "st%d" % R
@@ -439,6 +469,6 @@ def rank_program(g, core, T, topo):
     for k in range(2, 4):
         dma("a", T.osc[4 * k:4 * k + 4, :], T[fin + "s"][32 * k:32 * k + 4, PAD:PAD + TC], [fin + "0", fin + "1"], ["os%d" % k])
     op("g", None, extra=[("sent", sent)], dma=True)
-    op("a", None, ["oy0", "os0", "os1", "os2", "os3"], dma=True)
-    op("s", None, ["oc0", "oc1", "oy1", "lv0", "lv1", "lv2"], dma=True)
+    op("a", None, ["os0", "os1", "os2", "os3"], dma=True)
+    op("s", None, ["oc0", "oc1", "oy0", "oy1", "lv0", "lv1", "lv2"], dma=True)
     emit_program(ops, queues, T)

from concourse.bass import DstId, RemoteDMATransfer
from concourse.mybir import dt, AluOpType, AxisListType, ActivationFunctionType

ALU = AluOpType
ACT = ActivationFunctionType
R, L, TC, H, PAD = 3, 64, 384, 192, 2
X4, U8, BF, F32, I32, U16 = "float8_e4m3fn_x4", "uint8", "bfloat16", "float32", "int32", "uint16"

SCRATCH = {
    "psa": ("psum", [128, 2048], F32), "psb": ("psum", [128, 2048], F32),
    "tw": ("sbuf", [128, 4 * 580], BF), "hx": ("sbuf", [128, 4 * (TC + PAD)], BF),
    "bt": ("sbuf", [128, 4 * H], BF), "cg": ("sbuf", [128, 512], BF), "ci": ("sbuf", [128, 512], BF),
    "cl": ("sbuf", [128, 512], BF), "et": ("sbuf", [128, 520], BF), "et2": ("sbuf", [128, 520], BF),
    "vt": ("sbuf", [128, 512], BF), "zt": ("sbuf", [128, 512], BF), "jm": ("sbuf", [128, H], BF),
    "etr": ("sbuf", [128, 520], BF), "low": ("sbuf", [128, H], BF), "junk": ("sbuf", [128, 16], BF),
    "jnk2": ("sbuf", [128, H + PAD], BF), "d0": ("sbuf", [128, H], BF),
    "aip": ("sbuf", [128, 8], I32), "aik": ("sbuf", [128, 8], I32), "im": ("sbuf", [128, L], I32),
    "iv": ("sbuf", [128, L], I32), "iv2": ("sbuf", [128, L], I32),
    "ipen": ("sbuf", [128, 4], I32), "apen": ("sbuf", [128, 4], I32), "lc": ("sbuf", [128, 12], I32),
    "li": ("sbuf", [128, 24], I32),
    "f1": ("sbuf", [128, 8], F32), "f2": ("sbuf", [128, 8], F32), "col": ("sbuf", [128, 32], F32),
    "pen": ("sbuf", [128, 4], F32), "mc": ("sbuf", [128, 4], F32), "pc": ("sbuf", [128, 4], F32),
    "run": ("sbuf", [128, H + PAD], F32), "cnt": ("sbuf", [128, 12], F32),
    "ls": ("sbuf", [128, H], F32), "lf": ("sbuf", [128, 32], F32),
    "lt": ("sbuf", [128, 32], F32), "ysb": ("sbuf", [128, TC], F32), "dl": ("sbuf", [128, 4 * L], F32),
}


def _pair(name, n):
    SCRATCH[name + "q"] = ("sbuf", [128, n], X4)
    SCRATCH[name + "s"] = ("sbuf", [128, n], U8)


for _n, _w in (("w", 576), ("b", H), ("i", 128), ("cg", 128), ("ci", 128), ("cl", 128), ("e", 512), ("f", 512), ("z", 128)):
    _pair("k" + _n, _w)
for _t in range(R + 1):
    _pair("st%d" % _t, TC + PAD)
for _t in range(R):
    _pair("land%d" % _t, 384)
    _pair("val%d" % _t, 128)
    _pair("sel%d" % _t, TC)
    SCRATCH["ofr%d" % _t] = ("sbuf", [128, 4], U16)
    SCRATCH["ofl%d" % _t] = ("sbuf", [128, 24], U16)

NC, ND = 110, 22
SEMAPHORES = (["c%d" % k for k in range(NC)] + ["d%d" % k for k in range(ND)]
              + ["arr%d_%d" % (t, r) for t in range(R) for r in range(4)] + ["sent"])

BIT = 2.0 ** 26
FLOOR = -2.0 ** 70
MAGIC = 1.5 * 2.0 ** 28
CUT = (256, 192, 192, 160)


def exchange_plan(cores, topo):
    n = len(cores)
    plan = []
    for r, c in enumerate(cores):
        home = [k for k in range(n) if topo.chip(cores[k]) == topo.chip(c)]
        far = [k for k in range(n) if k not in home]
        i = home.index(r)
        early, late = far[i], far[1 - i]
        near = home[1 - i]
        held = None if late == n - 1 else n - 1
        pre = [1 - late] if late < 2 else sorted(range(late), key=lambda k: (k != r, k != near))
        post = [k for k in range(late, n) if k not in pre and k != held]
        if held is None or held == r:
            slots = [late] + [k for k in post[1:] if k != r] + [k for k in pre[::-1] if k != r]
        else:
            slots = [late] + [k for k in pre if k != r] + [held]
        out = topo.engines(c, cores[early])
        rest = [e for e in topo.engines(c, cores[near]) if e not in out]
        k = len(out) // 2
        tail = [("s", {early: out[:k], late: out[k:], near: rest}), ("q", {late: out})]
        calls = [[("q", {early: out}), ("q", {near: rest})] + tail] + [[("q", {early: out, near: rest})] + tail] * (R - 1)
        plan.append({"pre": pre, "post": post, "held": held, "slots": slots + [r], "calls": calls})
    return plan


def emit_program(ops, queues, T):
    writer, readers, known, issue, closure, waits, before = {}, {}, {}, [], [], [], {}
    for n, o in enumerate(ops):
        deps = set()
        for k in o["r"]:
            if k in writer: deps.add(writer[k])
        for k in o["w"]:
            if k in writer: deps.add(writer[k])
            deps.update(readers.get(k, ()))
        if o["cont"]:
            deps.discard(writer[o["w"][0]])
        kn = known.setdefault(o["q"], set())
        mine = []
        for d in sorted(deps, reverse=True):
            if d not in kn:
                mine.append(d)
                kn.add(d)
                kn.update(closure[d])
        waits.append(mine[::-1])
        issue.append(set(kn))
        c = set(kn)
        if not o["dma"]:
            if o["q"] in before:
                c.add(before[o["q"]])
                c.update(closure[before[o["q"]]])
            before[o["q"]] = n
        closure.append(c)
        for k in o["r"]: readers.setdefault(k, []).append(n)
        for k in o["w"]:
            writer[k] = n
            readers[k] = []
    signalled = set()
    for m in waits: signalled.update(m)
    pools = {False: ["c%d" % k for k in range(NC)], True: ["d%d" % k for k in range(ND)]}
    last, count, where = {}, {}, {}
    for n, o in enumerate(ops):
        q = queues[o["q"]]
        for d in waits[n]:
            q.wait_ge(T.sem[where[d][0]], where[d][1])
        for name, val in o["extra"]:
            q.wait_ge(T.sem[name], val)
        if o["f"] is None:
            continue
        ins = o["f"]()
        if n in signalled:
            name = [s for s in pools[o["dma"]] if s not in last or last[s] in issue[n]][0]
            step = 16 if o["dma"] else 1
            last[name] = n
            count[name] = count.get(name, 0) + step
            where[n] = (name, count[name])
            ins.then_inc(T.sem[name], step)


def rank_program(g, core, T, topo):
    rank = T.rank_of(core)
    if rank is None:
        return
    cores = list(T.cores)
    V, A, P, S = g.vector, g.scalar, g.tensor, g.sync
    queues = {"g": g, "v": V, "a": A, "p": P, "s": S}
    ops = []

    def op(q, f, r=(), w=(), dma=False, cont=False, extra=()):
        ops.append({"q": q, "f": f, "r": list(r), "w": list(w), "dma": dma, "cont": cont, "extra": list(extra)})

    def fill(ap, c, *keys):
        op("v", lambda: V.memset(ap, c), (), keys)

    def iota(ap, pattern, base, step, w, whole=False):
        if whole:
            op("g", lambda: g.iota(ap, pattern, base, step), [], w)
        else:
            op("g", lambda: g.iota(ap, pattern, base, step, allow_small_or_imprecise_dtypes=True), [], w)

    def ts(out, in0, s1, s2, op0, op1, r, w):
        if op1 is None:
            op("v", lambda: V.tensor_scalar(out, in0, s1, None, op0), r, w)
        else:
            op("v", lambda: V.tensor_scalar(out, in0, s1, s2, op0, op1), r, w)

    def tt(out, in0, in1, alu, r, w):
        op("v", lambda: V.tensor_tensor(out, in0, in1, alu), r, w)

    def copy(out, in_, r, w):
        op("v", lambda: V.tensor_copy(out, in_), r, w)

    def act(out, in_, func, r, w, **kw):
        op("a", lambda: A.activation(out, in_, func, **kw), r, w)

    def quant(name, a, b, tile, r, w):
        op("v", lambda: V.quantize_mx(T[name + "q"][:, a:b], T[name + "s"][:, a:b], tile), r, w)

    def bank(key):
        return (T.psa if key[0] == "A" else T.psb), 512 * int(key[1])

    def ps(key, a, b):
        buf, o = bank(key)
        return buf[:, o + a:o + b]

    def mm(key, wn, wa, xn, xa, n, start, stop, r, extra=()):
        op("p", lambda: P.matmul_mx(ps(key, 0, n), T[wn + "q"][:, wa:wa + 128], T[wn + "s"][:, wa:wa + 128],
                                    T[xn + "q"][:, xa:xa + n], T[xn + "s"][:, xa:xa + n], start, stop),
           r, [key], cont=not start, extra=extra)

    def dma(q, out, in_, r, w):
        op(q, lambda: queues[q].dma_start(out, in_), r, w, dma=True)

    def pick(dst, a, n, src, width, off, oa, r, w):
        o = T[off][:, oa:oa + n // 16]
        op("v", lambda: V.tensor_copy(T[dst + "q"][:, a:a + n].bitcast(dt.uint32),
                                      T[src + "q"][:, 0:width].bitcast(dt.uint32).indirect(o)), r, [w + "q"])
        op("a", lambda: A.activation(T[dst + "s"][:, a:a + n], T[src + "s"][:, 0:width].indirect(o), ACT.Copy), r, [w + "s"])

    tw, hx, col = T.tw, T.hx, T.col
    hxk = [["hx%d%d" % (h, b) for b in range(4)] for h in range(2)]
    PW, S1, R32, PW2R, PW2 = [col[:, 4 * k:4 * k + 1] for k in (0, 1, 2, 4, 5)]

    def zeros(out, w):
        act(out, tw[:, 16:272], ACT.Copy, ["z0"], w)

    def spread_w(t):
        for e in range(4):
            a = 4 * (196 + 128 * t) + e
            c = 4 * (68 + 8 * t + 6) + e
            act(tw[:, a:a + 253:4], tw[:, 16:80], ACT.Identity, ["z0", "wp"], ["w6%d%d" % (t, e)], bias=tw[:, c:c + 1])

    def quant_w6(t):
        a = 4 * (196 + 128 * t)
        quant("kw", 192 + 128 * t, 320 + 128 * t, tw[:, a:a + 512], ["w6%d%d" % (t, e) for e in range(4)] + ["z%d" % (t + 2)], ["kw%d" % (t + 1)])

    def zeros_w6(t):
        a = 4 * (196 + 128 * t + 64)
        zeros(tw[:, a:a + 256], ["z%d" % (t + 2)])

    def quant_state(t, h):
        a, b = (0, PAD + CUT[t]) if h == 0 else (PAD + CUT[t], PAD + TC)
        quant("st%d" % t, a, b, hx[:, 4 * a:4 * b], hxk[h] + (["hxpad"] if h == 0 else []), ["st%d%d" % (t, h)])

    def quant_e(name, tile, b):
        quant(name, 128 * b, 128 * b + 128, T[tile][:, 4 - b:516 - b], [tile], [name + str(b)])

    def member(h):
        p0, p1, a = 64 * h, 64 * h + 64, 256 * h
        ts(T.cg[p0:p1, a:a + 256:4], T.iv2[p0:p1, :], 16.0, col[p0:p1, 4:5], ALU.subtract, ALU.mult, ["iv2", "s1"], ["cg%d" % (2 * h)])
        ts(T.cg[p0:p1, a + 1:a + 256:4], T.iv2[p0:p1, :], col[p0:p1, 4:5], -0.5, ALU.mult, ALU.mult, ["iv2", "s1"], ["cg%d" % (2 * h + 1)])

    dma("a", tw[:, 272:368], T.w[:, 0:96], [], ["wp"])
    dma("s", hx[:, 8:8 + 4 * CUT[0]], T.x[:, 0:4 * CUT[0]], [], hxk[0])
    dma("s", hx[:, 8 + 4 * CUT[0]:8 + 4 * TC], T.x[:, 4 * CUT[0]:4 * TC], [], hxk[1])
    iota(T.aip[:, 0:6], [[1, 6]], 0, 1, ["aip"], True)
    iota(T.pc[:, 0:2], [[0, 2]], -15, 2, ["pc"])
    iota(T.im[:], [[1, L]], 0, 0, ["im"], True)
    iota(T.jm[:], [[0, 12], [-2, 16]], 0, 2, ["jm"])
    iota(T.etr[:], [[-1, 520]], 4, 4, ["etr"])
    iota(T.ipen[:], [[-16, 4]], 64, 1, ["ipen"], True)
    iota(T.d0[:], [[0, 12], [1, 16]], 0, 0, ["d0r"])
    aik = ["aik"]
    fill(tw[:, 0:272], 0.0, "z0", "it0", "it1", "it2a", "it2b")
    fill(tw[:, 368:784], 0.0, "z1")
    ts(T.aik[:, 0:6], T.aip[:, 0:6], 63, None, ALU.bitwise_and, None, ["aip"], aik)
    zeros_w6(0)
    zeros(T.cg[:, 0:256], ["cg0", "cg1"])
    zeros(T.cg[:, 256:512], ["cg2", "cg3"])
    fill(hx[:, 0:8], 0.0, "hxpad")
    ts(R32, T.pc[:, 0:1], MAGIC, MAGIC, ALU.add, ALU.subtract, ["pc"], ["r32"])
    ts(T.f1[:, 0:5], T.aik[:, 0:5], 5.0, 1.0, ALU.is_lt, ALU.add, aik, ["f1"])
    ts(S1, T.aik[:, 0:1], 6.0, 2.0 ** 42, ALU.is_lt, ALU.mult, aik, ["s1"])
    ts(T.f2[:, 0:5], T.aik[:, 0:5], 5.0, 1.0, ALU.is_ge, ALU.add, aik, ["f2"])
    op("v", lambda: V.tensor_reduce(PW, T.f1[:, 0:5], AxisListType.X, ALU.mult), ["f1"], ["pw"])
    fill(T.bt[:, 1:4 * H:2], BIT, "bt1")
    ts(T.iv[:], T.im[:], PW, None, ALU.mult, None, ["im", "pw"], ["iv"])
    ts(T.bt[:, 2:4 * H:4], T.jm[:], R32, BIT, ALU.is_equal, ALU.mult, ["jm", "r32"], ["bt2"])
    op("v", lambda: V.tensor_reduce(PW2R, T.f2[:, 0:5], AxisListType.X, ALU.mult), ["f2"], ["pw2r"])
    ts(T.iv2[:], T.iv[:], 32, None, ALU.bitwise_and, None, ["iv"], ["iv2"])
    spread_w(0)
    for e in (0, 1, 3):
        act(T.ci[:, e:512:4], T.bt[:, 2:512:4], ACT.Copy, ["bt2"], ["ci%d" % e], scale=1 / BIT)
    for h in range(2):
        act(T.ci[64 * h:64 * h + 64, 2:512:4], T.bt[64 * h:64 * h + 64, 2:512:4], ACT.Copy, ["bt2"], ["ci2%d" % h], scale=h * H / BIT)
    quant("kw", 0, 192, tw[:, 16:784], ["z0", "wp", "z1"], ["kw0"])
    member(0)
    quant_state(0, 0)
    quant_state(0, 1)
    dma("s", T.zt[:], T.z[:], ["st01"], ["zt"])
    member(1)
    quant_w6(0)
    act(T.et2[:], T.etr[:], ACT.Abs, ["etr"], ["et2"])
    act(T.et[:], T.et2[:], ACT.Relu, ["et2"], ["et"], scale=-0.125, bias=0.125)
    for k in range(2):
        zeros(T.cl[:, 256 * k:256 * k + 256], ["clz%d" % k])

    plan = exchange_plan(cores, topo)
    me = plan[rank]
    aside = me["held"] not in (None, rank)
    own = L * me["slots"].index(rank)
    sent = 0
    bts = ["bt0", "bt1", "bt2"]
    top = PAD + H - 1
    for t in range(R):
        st, nxt, land, val, sel = ["%s%d" % (s, k) for s, k in (("st", t), ("st", t + 1), ("land", t), ("val", t), ("sel", t))]
        ofr, ofl = "ofr%d" % t, "ofl%d" % t
        C = CUT[t + 1]
        span = ((0, C), (C, TC - C))
        both = [st + "0", st + "1"]
        kwp = ["kw0", "kw1"] if t else ["kw0"]
        kws = ["kw%d" % t, "kw%d" % (t + 1)]

        def pad_land():
            quant(land, 256, 384, tw[:, 528:1040], ["z1", "kw1"], [land + "pad"])

        def leaf_product():
            mm("A2", "kcl", 0, "kb", 0, H, True, True, ["kcl", "kb"])

        def leaf_scan():
            op("v", lambda: V.tensor_tensor_scan(T.ls[:], T.d0[:], ps("A2", 0, H), 0.0, ALU.mult, ALU.max), ["d0"], ["A2", "ls"])

        if t:
            quant_w6(t)
        mm("A0", "kw", 64 + 8 * t, st, PAD, H, True, False, kwp + [st + "0"])
        mm("A0", "kw", 8 * t, st, PAD + H, H, False, True, kwp + both)
        mm("A1", "kw", 192 + 128 * t, st, PAD, H, True, False, kws + both)
        mm("A1", "kw", 128 + 128 * t, st, PAD + H, H, False, False, kws + both)
        if t == 0:
            quant("kcg", 0, 128, T.cg[:], ["cg0", "cg1", "cg2", "cg3"], ["kcg"])
        ts(T.bt[:, 0:4 * H:4], ps("A0", 0, H), 0.0, BIT, ALU.is_lt, ALU.mult, [], ["A0", "bt0"])
        if t == 0:
            ts(T.apen[:], T.ipen[:], 48, None, ALU.bitwise_and, None, ["ipen"], ["apen"])
        quant("kb", 0, H, T.bt[:], bts, ["kb"])
        mm("A1", "kcg", 0, "kb", 0, H, False, True, ["kcg", "kb"])
        if t == 0:
            ts(T.pen[:], T.apen[:], 0.0, -2.0 ** 80, ALU.not_equal, ALU.mult, ["apen"], ["pen"])
            fill(T.low[:], FLOOR, "low")
            fill(T.run[:, 0:PAD], FLOOR, "runpad")
            fill(T.mc[:], 16.0, "mc")
        else:
            pad_land()
            leaf_product()
        op("v", lambda: V.tensor_tensor_scan(T.run[:, PAD:], ps("A1", 0, H), T.low[:], FLOOR, ALU.max, ALU.max), ["low"], ["A1", "run"])
        if t == 0:
            quant("kci", 0, 128, T.ci[:], ["ci0", "ci1", "ci20", "ci21", "ci3"], ["kci"])
        act(T.junk[:, 0:12], T.run[:, 15:top:16], ACT.Sign, ["run"], ["junk0", "hi"], bias=T.run[:, top:top + 1], scale=-1.0,
            accum_out=T.cnt[:, 4:5])
        act(T.jnk2[:], T.run[:], ACT.Sign, ["run", "runpad"], ["junk", "cnt"], bias=T.run[:, top:top + 1], scale=-1.0,
            accum_out=T.cnt[:, 0:1])
        ts(tw[0:64, 2:16:4], T.pen[0:64, :], T.run[0:64, top:top + 1], T.run[64:128, top:top + 1], ALU.add, ALU.is_ge,
           ["pen", "run"], ["it2a"])
        ts(tw[64:128, 2:16:4], T.pen[64:128, :], T.run[64:128, top:top + 1], T.run[0:64, top:top + 1], ALU.add, ALU.is_gt,
           ["pen", "run"], ["it2b"])
        ts(T.cnt[:, 8:9], T.cnt[:, 4:5], 16.0, None, ALU.mult, None, ["hi"], ["hi16"])
        ts(tw[:, 0:16:4], T.mc[:], T.cnt[:, 4:5], None, ALU.mult, None, ["mc", "hi"], ["it0"])
        ts(tw[:, 1:16:4], tw[:, 2:16:4], T.cnt[:, 0:1], T.cnt[:, 8:9], ALU.mult, ALU.subtract, ["cnt", "hi16", "it2a", "it2b"], ["it1"])
        quant("ki", 0, 128, tw[:, 0:512], ["it0", "it1", "it2a", "it2b", "z0", "z1", "wp"], ["ki"])
        mm("A3", "kci", 0, "ki", 0, 128, True, True, ["kci", "ki"])
        if t == 0:
            quant_e("ke", "et", 0)
            quant_e("ke", "et", 1)
        else:
            leaf_scan()
        copy(T[ofr][:], ps("A3", 0, 4), [], ["A3", ofr])
        pick(land, own, L, st, TC + PAD, ofr, 0, both + [ofr], land)
        for kind, peers in me["calls"][t]:
            trs = []
            for r in peers:
                pos = L * plan[r]["slots"].index(rank)
                rid, pid, _ = topo.addr(cores[r])
                src, dst = T[land + kind][:, own:own + L], T[land + kind][:, pos:pos + L]
                if kind == "q":
                    src, dst = src.bitcast(dt.uint8), dst.bitcast(dt.uint8)
                trs.append(RemoteDMATransfer(dst_ids=[DstId(rid=rid, pnc=pid)], dma_engine_mask=sum(1 << e for e in peers[r]),
                                             remote_sem=T.sem["arr%d_%d" % (t, rank)], src=src, dst=dst))
                sent += len(peers[r])
            op("g", lambda trs=trs: g.remote_dma_fused(trs, local_sem=T.sem.sent), [land + kind], [], dma=True)
        if t == 0:
            for h in range(2):
                ts(col[64 * h:64 * h + 64, 20:21], col[64 * h:64 * h + 64, 16:17], col[64 * h:64 * h + 64, 4:5], 2.0 ** (6 * h - 68),
                   ALU.mult, ALU.mult, ["pw2r", "s1"], ["pw2%d" % h])
            act(T.cl[32:48, 2:512:4], T.ci[32:48, 0:512:4], ACT.Identity, ["ci0", "clz0", "clz1"], ["cl2"], scale=2.0 ** -14, bias=-2.0 ** -14)
            act(T.cl[:, 0:512:4], T.ci[:, 0:512:4], ACT.Identity, ["ci0", "pw20", "pw21", "clz0", "clz1"], ["cl0"], scale=0.0, bias=PW2)
            act(T.d0[:], T.d0[:], ACT.Sign, ["d0r"], ["d0"])
            act(T.et2[:], T.et[:], ACT.Copy, ["et"], ["et2"], scale=-0.5)
            zeros(T.vt[:, 256:512], ["vtpad"])
            pad_land()
            quant_e("ke", "et", 2)
            quant_e("ke", "et", 3)
            quant("kcl", 0, 128, T.cl[:], ["cl0", "cl2"], ["kcl"])
            leaf_product()
            leaf_scan()
            quant_e("kf", "et2", 0)
        copy(T.lc[:], T.ls[:, 15:H:16], ["ls"], ["lc"])
        if t == 0:
            quant_e("kf", "et2", 1)
        if t == 1:
            quant("kz", 0, 128, T.zt[:], ["zt"], ["kz"])
        ts(T.li[:, 0:12], T.lc[:], 63, None, ALU.bitwise_and, None, ["lc"], ["li0"])
        ts(T.li[:, 12:24], T.lc[:], 6, None, ALU.logical_shift_right, None, ["lc"], ["li1"])
        if t == 0:
            quant_e("kf", "et2", 2)
            fill(T.lf[0:32, 24:32], 0.0, "lfpad")
        copy(T[ofl][:], T.li[:], ["li0", "li1"], [ofl])
        copy(T.lf[0:32, 0:24], T.li[0:32, :], ["li0", "li1"], ["lf"])
        if t == 0:
            quant_e("kf", "et2", 3)
        op("v", lambda: V.transpose(T.lt[0:32, :], T.lf[0:32, :]), ["lf", "lfpad"], ["lt"])
        if t < R - 1:
            zeros_w6(t + 1)
            spread_w(t + 1)

        seen = {rank}

        def unpack(r, b, start, stop, bk="B"):
            k = me["slots"].index(r)
            extra = [("arr%d_%d" % (t, o), sum(len(p.get(rank, ())) for _, p in plan[o]["calls"][t]))
                     for o in me["slots"][k:k + 2] if o not in seen]
            seen.update(me["slots"][k:k + 2])
            mm(bk + str(b), "ke", 128 * b, land, L * k, 128, start, stop, ["ke%d" % b, land + "q", land + "s", land + "pad"], extra)

        def hold(bk):
            for b in range(4):
                unpack(me["held"], b, True, True, bk)
            for b in range(4):
                act(T.dl[:, L * b:L * b + L], ps(bk + str(b), 0, L), ACT.Copy, [], [bk + str(b), "dl%d" % b])

        def load(h, bs):
            for b in bs:
                mm("AB"[h] + str(b), "ke", 128 * b, st, PAD + span[h][0], span[h][1], True, False, ["ke%d" % b] + both)

        if not aside:
            load(0, (0, 1, 3, 2))
        if me["held"] == rank:
            hold("B")
        for k, r in enumerate(me["pre"]):
            for b in range(4):
                unpack(r, b, k == 0, False)
            if aside and k == 0:
                hold("A")
        for b in range(4):
            for r in me["post"]:
                unpack(r, b, False, r == me["post"][-1])
            if me["held"] is not None:
                tt(T.vt[:, b:256:4], ps("B%d" % b, 0, L), T.dl[:, L * b:L * b + L], ALU.add, ["dl%d" % b], ["B%d" % b, "vt%d" % b])
            elif b % 2 == 0:
                act(T.vt[:, b:256:4], ps("B%d" % b, 0, L), ACT.Copy, [], ["B%d" % b, "vt%d" % b])
            else:
                copy(T.vt[:, b:256:4], ps("B%d" % b, 0, L), [], ["B%d" % b, "vt%d" % b])
        if aside:
            load(0, range(4))
        quant(val, 0, 128, T.vt[:], ["vt0", "vt1", "vt2", "vt3", "vtpad"], [val])
        dma("s", T.lv[t], T.lt[0:24, 0:16], ["lt", val], ["lv%d" % t])
        load(1, range(4))
        for h in range(2):
            pick(sel, span[h][0], span[h][1], val, L, ofl, span[h][0] // 16, [val, ofl], sel + str(h))
        for h in range(2):
            for b in range(4):
                mm("AB"[h] + str(b), "kf", 128 * b, sel, span[h][0], span[h][1], False, True,
                   ["kf%d" % b, sel + str(h) + "q", sel + str(h) + "s"])

        def drain(h, b):
            a, n = 4 * (PAD + span[h][0]) + b, span[h][1]
            k = "AB"[h] + str(b)
            if b % 2:
                act(hx[:, a:a + 4 * n - 3:4], ps(k, 0, n), ACT.Copy, [], [k, hxk[h][b]], scale=8.0)
            else:
                ts(hx[:, a:a + 4 * n - 3:4], ps(k, 0, n), 8.0, None, ALU.mult, None, [], [k, hxk[h][b]])

        for b in range(4):
            drain(0, b)
        if t < R - 1:
            for b in range(4):
                drain(1, b)
            quant_state(t + 1, 0)
        else:
            drain(1, 0)
            drain(1, 1)
            quant_state(t + 1, 0)
            dma("s", T.oc[:, 0:4 * C], T[nxt + "q"][:, PAD:PAD + C].bitcast(dt.uint8), [nxt + "0"], ["oc0"])
            mm("A0", "kz", 0, nxt, PAD, C, True, True, ["kz", nxt + "0"])
            drain(1, 2)
            drain(1, 3)
            act(T.ysb[:, 0:C], ps("A0", 0, C), ACT.Copy, [], ["A0", "y0"])
            dma("s", T.y[:, 0:C], T.ysb[:, 0:C], ["y0"], ["oy0"])
        quant_state(t + 1, 1)

    fin = "st%d" % R
    mm("A1", "kz", 0, fin, PAD + C, TC - C, True, True, ["kz", fin + "1"])
    dma("s", T.oc[:, 4 * C:4 * TC], T[fin + "q"][:, PAD + C:PAD + TC].bitcast(dt.uint8), [fin + "1"], ["oc1"])
    copy(T.ysb[:, C:TC], ps("A1", 0, TC - C), [], ["A1", "y1"])
    for k in range(2):
        dma("a", T.osc[4 * k:4 * k + 4, :], T[fin + "s"][32 * k:32 * k + 4, PAD:PAD + TC], [fin + "0", fin + "1"], ["os%d" % k])
    dma("s", T.y[:, C:TC], T.ysb[:, C:TC], ["y1"], ["oy1"])
    for k in range(2, 4):
        dma("a", T.osc[4 * k:4 * k + 4, :], T[fin + "s"][32 * k:32 * k + 4, PAD:PAD + TC], [fin + "0", fin + "1"], ["os%d" % k])
    op("g", None, extra=[("sent", sent)], dma=True)
    op("a", None, ["os0", "os1", "os2", "os3"], dma=True)
    op("s", None, ["oc0", "oc1", "oy0", "oy1", "lv0", "lv1", "lv2"], dma=True)
    emit_program(ops, queues, T)
